import numpy as np, ml_dtypes
CORES = [113,118,241,246]
N = 4
BF = ml_dtypes.bfloat16
P, L, B, T = 2048, 192, 1, 5
def skew(rng, n, hot):
    u = rng.random((N, 8, n))
    return np.take_along_axis(hot, np.minimum((P * u * u).astype(np.int64), P - 1), 2)
def parts(rng):
    x = rng.integers(0, 256, (N, 8, 16, P)); h = rng.integers(0, 256, (N, 8, 16, L))
    hot = np.argsort(rng.random((N, 8, P)), axis=2)
    pl = skew(rng, 16 * P, np.roll(hot, -1, axis=0)).reshape(N, 8, 16, P); kt = skew(rng, 16 * L, hot).reshape(N, 8, 16, L)
    nx = np.argsort(rng.random((N, 8, P)), axis=2); nx[:, 1::2] = skew(rng, P, hot)[:, 1::2]
    bm = rng.integers(0, P, (N, 8, L))
    th = np.stack([rng.integers(750, 1001, (N, 8)), rng.integers(900, 1251, (N, 8))], axis=2)
    return x, pl, nx, kt, h, bm, th
def pack(x, pl, nx, kt, h, bm, th):
    return {"xp": np.ascontiguousarray(x.reshape(N, 128, P)).astype(np.float32).astype(BF), "pl": np.ascontiguousarray(pl.reshape(N, 128, P)).astype(np.int32), "nx": np.ascontiguousarray(nx).astype(np.int32),
            "kt": np.ascontiguousarray(kt.reshape(N, 128, L)).astype(np.int32), "hm": np.ascontiguousarray(h.reshape(N, 128, L)).astype(np.float32).astype(BF), "bm": np.ascontiguousarray(bm).astype(np.int32), "th": np.ascontiguousarray(th).astype(np.int32)}
def setup_inputs(rng):
    return pack(*parts(rng))
def setup_inputs_spread(rng):
    x, pl, nx, kt, h, bm, th = parts(rng)
    x = np.minimum((rng.random(x.shape) * np.exp2(8.1 * rng.random((N, 8, 1, P)))).astype(np.int64), 255)
    h = np.minimum((rng.random(h.shape) * np.exp2(8.1 * rng.random((N, 8, 1, L)))).astype(np.int64), 255)
    th = np.minimum(np.exp2(12.0 * rng.random((N, 8, 2))).astype(np.int64), 4095); th[:, 2, 0] = rng.integers(300, 1200, N)
    hot = np.argsort(rng.random((N, 8, P)), axis=2); u = rng.random((N, 8, 16 * P)) ** 4
    pl = np.take_along_axis(np.roll(hot, -1, axis=0), np.minimum((P * u).astype(np.int64), P - 1), 2).reshape(N, 8, 16, P)
    nx[:, ::3] = skew(rng, P, hot)[:, ::3]
    return pack(x, pl, nx, kt, h, bm, th)
def edge(rng, n):
    return np.where(rng.random((N, 8, n)) < 0.7, (P - 1) * rng.integers(0, 2, (N, 8, n)), rng.integers(0, P, (N, 8, n)))
def setup_inputs_ends(rng):
    k = rng.integers(0, 5, (N, 8, 1, P)); x = np.where(k == 0, 0, np.where(k == 1, 255, 255 * rng.integers(0, 2, (N, 8, 16, P))))
    k = rng.integers(0, 8, (N, 8, 1, L)); h = np.where(k == 0, 0, np.where(k == 1, 255, np.where(k == 2, 127, 255 * rng.integers(0, 2, (N, 8, 16, L)))))
    x[..., 0] = 0; x[..., P - 1] = 255
    pl = edge(rng, 16 * P).reshape(N, 8, 16, P); kt = edge(rng, 16 * L).reshape(N, 8, 16, L); nx = edge(rng, P); bm = edge(rng, L)
    th = 4095 * np.ones((N, 8, 2), np.int64); th[:, :, 1] = 4095 * rng.integers(0, 2, (N, 8))
    for q in range(N):
        o = rng.permutation(7); th[q, o[:2], 0] = 0; th[q, o[2], 1] = 0; th[q, 7, 1] = 4095
        for g in range(8):
            if (q + g) % 4 == 0: nx[q, g, 0] = P - 1; nx[q, g, P - 1] = 0
            else: nx[q, g, 0] = rng.integers(7, P - 1); nx[q, g, P - 1] = rng.integers(7, P - 1)
        for g in (int(o[3]), 7):
            a = x[q, g]; a[:, [P - 1, 1, 2, 3]] = 255; a[:, [0, 4, 5, 6]] = 0
            kt[q, g, :, L - 1] = np.tile(np.array([P - 1, 1, 2, 3]), 4); h[q, g, :, L - 1] = 0
            kt[q, g, :, L - 2] = np.tile(np.array([5, 0, 4, 6]), 4); h[q, g, :, L - 2] = 255
    return pack(x, pl, nx, kt, h, bm, th)
def setup_inputs_corners(rng):
    x, pl, nx, kt, h, bm, th = parts(rng); pp = np.arange(P); kk = np.arange(16)[:, None]; li = np.arange(L)[None, :]
    for q in range(N):
        for g in range(8):
            b = (q - 1) % N; w = (g + q) % 8
            if w == 0: nx[q, g] = pp; th[q, g] = (4095, 4095)
            elif w == 1: nx[q, g] = pp ^ 1; th[q, g] = (1200, 0)
            elif w == 2:
                nx[q, g] = (pp + 1) % P; kt[q, g] = (P - 40 + li + kk) % P; pl[b, g] = (pp[None, :] + kk) % P; th[q, g] = (4095, 4095)
            elif w == 3:
                nx[q, g] = P - 1; bm[q, g] = np.where(li[0] % 3 == 0, 0, np.where(li[0] % 3 == 1, P - 1, li[0])); th[q, g] = (2000, 4095)
            elif w == 4:
                z = (0, P - 1, P // 2)[q % 3]; kt[q, g] = z; pl[b, g] = z; th[q, g] = (4095, 1100)
            elif w == 5:
                x[q, g] = x[q, g][:, pp - (pp & 7)]; th[q, g] = (2000, 1000)
                kt[q, g] = 8 * rng.integers(0, P // 8, (1, L)) + rng.integers(0, 8, (16, L)); pl[b, g] = 8 * rng.integers(0, P // 8, (1, P)) + rng.integers(0, 8, (16, P))
            elif w == 6:
                th[q, g] = (0, 4095); bm[q, g, 0] = 0; bm[q, g, L - 1] = P - 1; nx[q, g, 0] = 0
            else:
                kt[q, g] = (li + kk) & 15; pl[b, g] = rng.integers(0, 16, (16, P)); nx[q, g, :16] = (np.arange(16) + 1) & 15; th[q, g] = (4095, 4095)
    x[:, 7] = 255; h[:, 7] = 255; nx[:, 7] = pp; th[:, 7] = 4095
    kt[:, 7] = np.where(li < 31, 16 + li, (li + kk) & 15); pl[:, 7] = kk; pl[:, 7, :, 16:47] = 64 + np.arange(31)
    for q in range(N):
        b = (q - 1) % N; assert np.sum(np.any(~np.isin(pl[b, 7][:, kt[b, 7, 0]], kt[q, 7, 0]), axis=0)) == 31
    return pack(x, pl, nx, kt, h, bm, th)
def setup_inputs_ties(rng):
    x, pl, nx, kt, h, bm, th = parts(rng); t = rng.integers(40, 101, (N, 8, 1))
    far = t + np.where(rng.random((N, 8, P)) < 0.5, rng.integers(-1, 2, (N, 8, P)), rng.integers(0, 34, (N, 8, P)))
    x = 100 + np.where(np.arange(16)[:, None] == rng.integers(0, 16, (N, 8, 1, P)), far[:, :, None, :], 0)
    h = 100 + np.zeros((N, 8, 16, L), np.int64); h[:, :, 0] += (rng.random((N, 8, L)) < 0.125).astype(np.int64)
    order = np.argsort(far + rng.random(far.shape), axis=2); q = np.array([0.0, 0.2, 0.35, 0.55, 0.7, 0.9])
    def near(n, o):
        a = (P * rng.choice(q, (N, 8, 1, n))).astype(np.int64); i = np.minimum(a + ((P - a) * rng.random((N, 8, 16, n))).astype(np.int64), P - 1)
        return np.take_along_axis(o, i.reshape(N, 8, 16 * n), 2).reshape(N, 8, 16, n)
    kt = near(L, order); pl = near(P, np.roll(order, -1, axis=0))
    th = np.concatenate([t, ((t - 1) >> 1) + t + rng.integers(-1, 2, (N, 8, 1))], axis=2)
    return pack(x, pl, nx, kt, h, bm, th)
def sums(d):
    return (d[None, :] + ((np.arange(16)[:, None] + np.arange(d.shape[0])[None, :]) & 15)) >> 4
def setup_inputs_counts(rng):
    x, pl, nx, kt, h, bm, th = parts(rng); li = np.arange(L); kk = np.arange(16)[:, None]; gs = [int(g) for g in rng.permutation(8)]
    o = np.argsort(rng.random((N, 8, P)), axis=2)[:, :, :5 * L].reshape(N, 8, 5, L)
    h[:, gs[:6]] = 0
    for w in range(5):
        g = gs[w]; r = rng.permutation(L)
        for q in range(N):
            a, b, c, e, f = o[q, g]; a2, b2, c2, e2, f2 = o[(q + 1) % N, g]; pq = pl[q, g]; nq = nx[q, g]; kq = kt[q, g]
            if w < 2: t = 16 * int(rng.integers(128, 250)) + int(rng.choice(np.array([3, 4, 5, 11, 12, 13])))
            else: t = int(rng.integers(64, 4001))
            d = t + 40 + rng.integers(0, 41, P)
            if w == 0:
                d = t - 17 + rng.integers(0, 35, P); d[a] = t - 17 + li % 35; kq[:] = a; th[q, g, 0] = t
            elif w == 1:
                d = rng.integers(0, 4081, P); d[a] = 0; d[b] = t - 17 + li % 35; nq[a] = b; kq[:] = a; th[q, g] = (int(rng.integers(64, 4001)), t)
            elif w == 2:
                d[a] = 0; d[b] = t - 2 + li % 36; nq[a] = f; pq[:, a] = b2; kq[:] = a; th[q, g] = (t, 0)
            elif w == 3:
                m = r[:40]; v = r[40:53]
                d[a] = 0; d[b] = 0; d[c[m]] = t - 2 + np.arange(40) % 36
                nq[a] = f; nq[b] = f; nq[a[v]] = a[v]
                pq[:, a] = f2; pq[:, a[m]] = b2[m]; pq[:, a[v]] = a2[v][(np.arange(13) + kk) % 13]; pq[:, b[m]] = c2[m]
                kq[:] = a; th[q, g] = (t, 0)
            else:
                m = r[:52]; z = r[52:]
                d[a[m]] = 0; d[e[z]] = t - 2 + np.arange(L - 52) % 36
                nq[a[m[:-1]]] = a[m[1:]]; nq[a[m[-1]]] = f[0]; nq[b] = c; bm[q, g] = b
                pq[:, a] = f2; pq[:, b] = f2; pq[:, f] = f2; pq[:, c] = e2
                kq[:] = f; kq[:, m] = a[m]; th[q, g] = (t, 0)
            x[q, g] = sums(d)
    g = gs[5]; x[:, g] = 0; nx[:, g] = np.arange(P); th[:, g] = 4095
    kt[:, g] = np.where(li[None, :] < 31, 16 + li[None, :], (li[None, :] + kk) & 15); pl[:, g] = kk; pl[:, g, :, 16:47] = 64 + np.arange(31)
    return pack(x, pl, nx, kt, h, bm, th)
def check_inputs(d):
    bad = []
    for k, hi in (("xp", 255), ("pl", P - 1), ("nx", P - 1), ("kt", P - 1), ("hm", 255), ("bm", P - 1), ("th", 4095)):
        v = np.asarray(d[k]).astype(np.float64)
        if not (np.min(v) >= 0 and np.max(v) <= hi): bad.append("range of " + k)
        if k in ("xp", "hm") and np.any(v != np.floor(v)): bad.append("whole numbers of " + k)
    return bad
def pick(a, ix):
    return np.take_along_axis(a, ix[:, :, None, :], 3)
def mark(flags, y, go):
    a, g, i = np.nonzero(go); flags[a, g, y[a, g, i]] = True
def reference(xp, pl, nx, kt, hm, bm, th):
    x = xp.astype(np.float32).astype(np.int64).reshape(N, 8, 16, P); par = pl.astype(np.int64).reshape(N, 8, 16, P); nxt = nx.astype(np.int64)
    k = kt.astype(np.int64).reshape(N, 8, 16, L); h = hm.astype(np.float32).astype(np.int64).reshape(N, 8, 16, L)
    b = bm.astype(np.int64); t1 = th.astype(np.int64)[:, :, 0:1]; t2 = th.astype(np.int64)[:, :, 1:2]
    j = np.tile(np.arange(P, dtype=np.int64), (N, 8, 1)); eaten = np.zeros((N, 8, P), bool); a = np.zeros((N, 8, 1), np.int64)
    for t in range(T):
        c = np.take_along_axis(j, k.reshape(N, 8, 16 * L), 2).reshape(N, 8, 16, L)
        void = np.take_along_axis(eaten, c.reshape(N, 8, 16 * L), 2).reshape(N, 8, 16, L)
        d = np.stack([np.add.reduce(np.abs(pick(x, c[:, :, i]) - h), axis=2) for i in range(16)], axis=2)
        d = np.where(void, 2 ** 20, d)
        w = np.argmin(d, axis=2)[:, :, None, :]
        hit = np.take_along_axis(d, w, 2)[:, :, 0] < t1 + (a & 31)
        y = np.where(hit, np.take_along_axis(c, w, 2)[:, :, 0], np.take_along_axis(j, b, 2))
        new = np.zeros((N, 8, P), bool); go = hit
        h = np.where(go[:, :, None, :], (h + pick(x, y)) >> 1, h); mark(new, y, go)
        for s in range(B):
            n = np.take_along_axis(j, np.take_along_axis(nxt, y, 2), 2); xn = pick(x, n)
            go = go & ~np.take_along_axis(eaten, n, 2) & (np.add.reduce(np.abs(xn - h), axis=2) <= t2)
            y = np.where(go, n, y); h = np.where(go[:, :, None, :], (h + xn) >> 1, h); mark(new, y, go)
        b = np.take_along_axis(nxt, y, 2); a = np.add.reduce(hit.astype(np.int64), axis=2, keepdims=True)
        j = np.where(new, nxt, j); eaten = eaten | new
        j = np.take_along_axis(j, j, 2)
        if t < T - 1:
            k = np.roll(pick(par, y), 1, axis=0); h = np.roll(h, 1, axis=0)
    return {"yj": j.astype(np.float32), "yh": h.reshape(N, 128, L).astype(np.float32).astype(BF), "yb": b.astype(np.float32)}

@@ -1,0 +1,546 @@
+from concourse.mybir import AluOpType as Op, ActivationFunctionType as Act
+
+BIG = 1.0e9
+L, P, NV = 192, 2048, 5
+HS = P
+VO = P + L
+TW = VO + 16
+NX = 144
+CB = L - NX
+CHUNKS = (0, 48, 104, 144)
+QW = 130
+NA = 20
+ORDER = list(range(12)) + list(range(NA, 24)) + list(range(12, NA))
+GK = 9
+
+B16, F32, I32, U16 = "bfloat16", "float32", "int32", "uint16"
+SCRATCH = {
+    "TX": ("sbuf", [128, TW], B16), "XV": ("sbuf", [128, P], B16), "TF": ("sbuf", [128, TW], B16),
+    "BB": ("sbuf", [128, P], B16), "B1": ("sbuf", [128, P], B16), "PL": ("sbuf", [128, P], I32),
+    "HX": ("sbuf", [128, NX * 16], B16), "DX": ("sbuf", [128, NX * 16], B16), "AX": ("sbuf", [128, NX * 16], B16),
+    "GB": ("sbuf", [128, CB * 16], B16), "AB": ("sbuf", [128, CB * 16], B16),
+    "KI": ("sbuf", [128, L], I32), "KA": ("sbuf", [128, 2 * L], I32), "KAB": ("sbuf", [128, 2 * L], F32),
+    "VT": ("sbuf", [128, 2 * L], F32), "MS": ("sbuf", [128, 2 * L], F32), "RST": ("sbuf", [128, 2 * L], F32), "RS0": ("sbuf", [128, 2 * L], F32),
+    "MI": ("sbuf", [128, 24], I32), "ML": ("sbuf", [128, 24], I32), "LB": ("sbuf", [128, 24], B16), "MV": ("sbuf", [128, 12], B16),
+    "L1f": ("sbuf", [128, 12], F32), "L1": ("sbuf", [128, 12], U16), "MISS": ("sbuf", [128, 12], F32), "CI": ("sbuf", [128, 12], F32),
+    "SI": ("sbuf", [128, L], I32), "Q1": ("sbuf", [128, L], I32), "FF": ("sbuf", [128, 3 * L], B16),
+    "M1": ("sbuf", [128, 12], U16), "E2": ("sbuf", [128, L], B16), "AE": ("sbuf", [128, L], B16), "F2": ("sbuf", [128, L], I32),
+    "BR": ("sbuf", [128, L], B16), "QR": ("sbuf", [128, 48], F32), "BRL": ("sbuf", [128, 12], F32),
+    "BY": ("sbuf", [128, 12], F32), "BN": ("sbuf", [128, 12], F32), "YM": ("sbuf", [128, 24], F32),
+    "YF": ("sbuf", [128, 12], F32), "YU": ("sbuf", [128, 12], U16), "BF": ("sbuf", [128, 12], F32), "BU": ("sbuf", [128, 12], U16),
+    "JB": ("sbuf", [128, 24], F32), "FB": ("sbuf", [128, L], B16),
+    "OR": ("sbuf", [128, 24 * 128], B16), "OQ": ("sbuf", [128, 24 * QW], B16), "CS": ("sbuf", [128, 128], F32),
+    "MK": ("sbuf", [128, 128], B16), "JL": ("sbuf", [128, 128], F32), "NL": ("sbuf", [128, 128], F32),
+    "ZF": ("sbuf", [128, 128], F32), "ZU": ("sbuf", [128, 128], U16), "JU": ("sbuf", [128, 128], U16),
+    "AI": ("sbuf", [128, 2], I32), "AJ": ("sbuf", [128, 2], I32), "AK": ("sbuf", [128, 2], F32), "THR": ("sbuf", [128, 2], F32),
+    "T1K": ("sbuf", [128, 2], F32), "T2": ("sbuf", [128, 2], F32),
+    "ROW": ("sbuf", [128, P], F32), "RB": ("sbuf", [128, 4 * L], F32),
+    "BD": ("sbuf", [128, 128], B16), "ONE": ("sbuf", [128, 128], B16), "ON2": ("sbuf", [128, L], B16),
+    "ID": ("sbuf", [128, 128], B16), "NI": ("sbuf", [128, 128], B16), "SP": ("sbuf", [128, 128], B16), "SM": ("sbuf", [128, 128], B16),
+    "N32": ("sbuf", [128, 128], B16), "KBM": ("sbuf", [128, 128], B16), "BO": ("sbuf", [128, 128], B16),
+    "WYR": ("sbuf", [128, 128], B16), "WNR": ("sbuf", [128, 128], B16), "IQ": ("sbuf", [128, 129], B16),
+    "SU": ("sbuf", [128, 2048], B16), "SY": ("sbuf", [128, 2048], B16), "SN": ("sbuf", [128, 2048], B16), "SQ": ("sbuf", [128, 2048], B16),
+    "SR": ("sbuf", [128, 2048], B16), "MT": ("sbuf", [128, 2048], B16), "PP": ("sbuf", [128, 12 * 128], B16),
+    "CO": ("sbuf", [128, 16], F32), "CT": ("sbuf", [128, 16], F32), "RC": ("sbuf", [128, 16], F32), "R16": ("sbuf", [128, 16], F32),
+    "IP": ("sbuf", [128, 2], I32), "IW": ("sbuf", [128, 2], I32), "IL": ("sbuf", [128, 128], I32), "I12": ("sbuf", [128, 12], I32), "IC": ("sbuf", [128, 128], I32),
+    "CF": ("sbuf", [128, 4 * 128], B16), "CW": ("sbuf", [128, 4 * 128], I32), "NXC": ("sbuf", [128, 128], I32), "ICm": ("sbuf", [128, 128], I32),
+    "BMC": ("sbuf", [128, 12], I32), "BMw": ("sbuf", [128, 24], I32), "BMf": ("sbuf", [128, 24], B16), "BMR": ("sbuf", [128, L], B16),
+    "TH": ("sbuf", [128, 2], I32), "THw": ("sbuf", [128, 4], I32), "THf": ("sbuf", [128, 4], B16),
+    "TSR": ("sbuf", [128, 128], B16), "TSx": ("sbuf", [128, 128], B16), "TS0": ("sbuf", [128, 128], B16), "TS1": ("sbuf", [128, 128], B16),
+    "TMP": ("sbuf", [128, 512], B16),
+    "HH": ("sbuf", [128, 2 * NV * L], B16), "KK": ("sbuf", [128, 2 * NV * L], U16),
+}
+ALIAS = {}
+for _t in range(NV):
+    ALIAS["H%d" % _t] = ("HH", L * _t, L)
+    ALIAS["HS%d" % _t] = ("HH", L * (NV + _t), L)
+    ALIAS["K%d" % _t] = ("KK", L * _t, L)
+    ALIAS["KS%d" % _t] = ("KK", L * (NV + _t), L)
+for _k, _n in enumerate(("BD0", "BD1", "N3a", "N3b")):
+    ALIAS[_n] = ("TMP", 128 * _k, 128)
+for _k, _n in enumerate(("FY", "FN", "GF")):
+    ALIAS[_n] = ("FF", L * _k, L)
+for _t in range(8):
+    SCRATCH["p%d" % _t] = ("psum", [128, 512], F32)
+NDMA = 24
+SEMAPHORES = ["sV", "sA", "sT", "sG", "loc"] + ["d%d" % k for k in range(NDMA)] + ["ha%d" % t for t in range(1, NV)] + ["ka%d" % t for t in range(1, NV)]
+
+
+def make_emitter(g, T):
+    queues = {"V": g.vector, "A": g.scalar, "T": g.tensor, "G": g, "S": g.sync, "C": g.scalar}
+    hist, know, snap, count, nd = {}, {}, {}, {}, [0]
+
+    def ap(r):
+        name, c0, c1, st, p = r
+        return T[name][p, c0:c1:st] if st != 1 else T[name][p, c0:c1]
+
+    def clash(a, b):
+        if a[1] >= b[2] or b[1] >= a[2]:
+            return False
+        if a[3] == b[3] and a[3] > 1 and (a[1] - b[1]) % a[3]:
+            return False
+        if a[4] != b[4] and a[4].step is not None and a[4].step == b[4].step and a[4].start != b[4].start:
+            return False
+        return True
+
+    def await_(q, sem, val):
+        k = know.setdefault(q, {})
+        if k.get(sem, 0) >= val:
+            return
+        queues[q].wait_ge(T.sem[sem], val)
+        for s, v in snap.get((sem, val), {}).items():
+            if v > k.get(s, 0):
+                k[s] = v
+        k[sem] = val
+
+    def deps(q, reads, writes):
+        need = {}
+        for w, rs in ((False, reads), (True, writes)):
+            for r in rs:
+                psum = SCRATCH.get(r[0], ("",))[0] == "psum"
+                for (h, hw, hq, sem, val) in hist.get(r[0], []):
+                    if psum and hq != q:
+                        hit = True
+                    else:
+                        hit = (w or hw) and clash(r, h)
+                        if hit and psum and q == "T":
+                            hit = False
+                    if hit and val > need.get(sem, 0):
+                        need[sem] = val
+        for sem in sorted(need):
+            await_(q, sem, need[sem])
+
+    def note(q, reads, writes, sem, val):
+        for w, rs in ((False, reads), (True, writes)):
+            for r in rs:
+                h = hist.setdefault(r[0], [])
+                if w and r[0][0] != "p":
+                    h[:] = [e for e in h if not (r[1] <= e[0][1] and r[2] >= e[0][2] and r[3] == 1 and r[4] == slice(None) and (e[2] != q or e[1]))]
+                h[:] = [e for e in h if not (e[2] == q and e[1] == w and e[0] == r)]
+                h.append((r, w, q, sem, val))
+
+    def op(q, fn, reads, writes):
+        deps(q, reads, writes)
+        sem = "s" + q
+        count[q] = count.get(q, 0) + 1
+        fn(queues[q]).then_inc(T.sem[sem], 1)
+        k = dict(know.setdefault(q, {}))
+        k[sem] = count[q]
+        snap[(sem, count[q])] = k
+        note(q, reads, writes, sem, count[q])
+
+    def dma(q, out, in_, reads, writes):
+        kq = "A" if q == "C" else q
+        deps(kq, reads, writes)
+        sem = "d%d" % nd[0]
+        nd[0] += 1
+        queues[q].dma_start(out, in_).then_inc(T.sem[sem], 16)
+        snap[(sem, 16)] = dict(know.setdefault(kq, {}))
+        note("D" + sem, reads, writes, sem, 16)
+
+    def arrive(name, sem, val):
+        note("R" + sem, [], [R(name)], sem, val)
+
+    def finish():
+        for q in ("V", "A", "T", "G"):
+            if count.get(q):
+                await_("G", "s" + q, count[q])
+        for k in range(nd[0]):
+            await_("G", "d%d" % k, 16)
+
+    return ap, op, dma, arrive, deps, finish
+
+
+def R(name, c0=0, c1=None, st=1, p=slice(None)):
+    if name in ALIAS:
+        base, off, w = ALIAS[name]
+        return (base, off + c0, off + (w if c1 is None else c1), st, p)
+    return (name, c0, SCRATCH[name][1][1] if c1 is None else c1, st, p)
+
+
+def col(name, j):
+    return R(name, j, j + 1)
+
+
+def rank_program(g, core, T, topo):
+    rank = T.rank_of(core)
+    if rank is None:
+        return
+    n = len(T.cores)
+    nxt, prv = T.cores[(rank + 1) % n], T.cores[(rank - 1) % n]
+    rid, pid = topo.addr(nxt, core)
+    mask = topo.mask(core, nxt)
+    ap, op, dma, arrive, deps, finish = make_emitter(g, T)
+
+    def tt(out, a, b, o):
+        op("V", lambda e: e.tensor_tensor(ap(out), ap(a), ap(b), o), [a, b], [out])
+
+    def ts(out, a, s1, o0, s2=None, o1=None):
+        rd = [a] + [s for s in (s1, s2) if isinstance(s, tuple)]
+        v1 = ap(s1) if isinstance(s1, tuple) else s1
+        v2 = ap(s2) if isinstance(s2, tuple) else s2
+        if o1 is None:
+            op("V", lambda e: e.tensor_scalar(ap(out), ap(a), v1, None, o0), rd, [out])
+        else:
+            op("V", lambda e: e.tensor_scalar(ap(out), ap(a), v1, v2, o0, o1), rd, [out])
+
+    def cp(out, a):
+        op("V", lambda e: e.tensor_copy(ap(out), ap(a)), [a], [out])
+
+    def fill(out, c):
+        op("V", lambda e: e.memset(ap(out), c), [], [out])
+
+    def act(out, a, f=Act.Copy):
+        op("A", lambda e: e.activation(ap(out), ap(a), f), [a], [out])
+
+    def act_bias(out, a, f, b):
+        op("A", lambda e: e.activation(ap(out), ap(a), f, bias=ap(b)), [a, b], [out])
+
+    def act_lin(out, a, sc, bs):
+        op("A", lambda e: e.activation(ap(out), ap(a), Act.Copy, bias=bs, scale=sc), [a], [out])
+
+    def act_scale(out, a, c):
+        op("A", lambda e: e.activation(ap(out), ap(a), Act.Copy, scale=ap(c)), [a, c], [out])
+
+    def vgather(out, win, off):
+        op("V", lambda e: e.tensor_copy(ap(out), ap(win).indirect(ap(off))), [win, off], [out])
+
+    def agather(out, win, off):
+        op("A", lambda e: e.activation(ap(out), ap(win).indirect(ap(off)), Act.Copy), [win, off], [out])
+
+    def ttgather(out, win, off, b, o):
+        op("V", lambda e: e.tensor_tensor(ap(out), ap(win).indirect(ap(off)), ap(b), o), [win, off, b], [out])
+
+    def mm(out, lhs, rhs, start=True, stop=True):
+        op("T", lambda e: e.matmul(ap(out), ap(lhs), ap(rhs), start, stop), [lhs, rhs], [out])
+
+    def iota(out, pat, base, cm):
+        small = SCRATCH[out[0]][2] != I32
+        op("G", lambda e: e.iota(ap(out), pat, base, cm, allow_small_or_imprecise_dtypes=True) if small else e.iota(ap(out), pat, base, cm), [], [out])
+
+    def asel(out, a, pat, o, fv, base, cm):
+        op("G", lambda e: e.affine_select(ap(out), ap(a), pat, o, fv, base, cm), [a], [out])
+
+    def lists(out, S, src, width):
+        for r in range(16):
+            mm(R(out[0], out[1], out[1] + width), R(S, 128 * r, 128 * r + 128), R(src, r, 16 * width, 16), r == 0, r == 15)
+
+    def lists2(bank, c, S, width):
+        for r in range(16):
+            mm(R(bank, c, c + width), R(S, 128 * r, 128 * r + 128), R("FF", r, 16 * width, 16), r == 0, r == 15)
+
+    DJ = R("p2", 384, 512)
+
+    dma("S", T["KI"][:, :], T["kt"][:, :], [], [R("KI")])
+    dma("C", T["NXC"][:, :], T["nx"][:, :], [], [R("NXC")])
+    dma("S", ap(R("H0")), T["hm"][:, :], [], [R("H0")])
+    dma("S", T["TX"][:, 0:P], T["xp"][:, :], [], [R("TX", 0, P)])
+    dma("C", T["TH"][0:8, :], T["th"][:, :], [], [R("TH")])
+    dma("C", T["BMC"][:, :], T["bm"][:, :], [], [R("BMC")])
+    dma("S", T["XV"][:, :], T["xp"][:, :], [], [R("XV")])
+    dma("S", T["PL"][:, :], T["pl"][:, :], [], [R("PL")])
+
+    fill(R("ONE"), 1.0)
+    fill(R("ON2"), 1.0)
+    iota(R("IP"), [[0, 2]], 0, 1)
+    iota(R("BD0"), [[0, 8], [1, 16]], 0, 0)
+    asel(R("BD1"), R("BD0"), [[-16, 8], [0, 16]], Op.is_ge, -1.0, 0, 1)
+    asel(R("BD"), R("BD1"), [[16, 8], [0, 16]], Op.is_ge, -1.0, 15, -1)
+    asel(R("ID"), R("ONE"), [[-1, 128]], Op.is_equal, 0.0, 0, 1)
+    iota(R("IC"), [[1, 128]], 0, 128)
+    iota(R("I12"), [[16, 12]], P, 0)
+    asel(R("SP"), R("ONE"), [[-1, 128]], Op.is_equal, 0.0, 16, 1)
+    asel(R("SM"), R("ONE"), [[-1, 128]], Op.is_equal, 0.0, -16, 1)
+    e8 = slice(0, 8)
+    asel(R("TSx", p=e8), R("ONE", p=e8), [[1, 128]], Op.is_ge, 0.0, 0, -16)
+    asel(R("TSR", p=e8), R("TSx", p=e8), [[-1, 128]], Op.is_ge, 0.0, 15, 16)
+    asel(R("TS0", p=e8), R("ONE", p=e8), [[-2, 4], [0, 32]], Op.is_equal, 0.0, 0, 1)
+    asel(R("TS1", p=e8), R("ONE", p=e8), [[-2, 4], [0, 32]], Op.is_equal, 0.0, -1, 1)
+    iota(R("IQ"), [[1, 129]], -129, 0)
+    iota(R("R16"), [[1, 16]], 0, 0)
+    iota(R("IL"), [[16, 128]], 0, 0)
+    asel(R("N3a"), R("ONE"), [[-32, 4], [0, 32]], Op.is_ge, 0.0, 0, 1)
+    asel(R("N3b"), R("N3a"), [[32, 4], [0, 32]], Op.is_ge, 0.0, 31, -1)
+
+    PM, RM1, RM0 = col("CO", 0), col("CO", 1), col("CO", 2)
+    WY, WN, WQ, WR, K64, W140 = (col("CO", j) for j in range(3, 9))
+    ts(R("IW", 0, 1), R("IP", 0, 1), 15, Op.bitwise_and)
+    ts(R("IW", 1, 2), R("IP", 1, 2), 31, Op.bitwise_and)
+    cp(PM, R("IW", 0, 1))
+    for j, (f, w) in enumerate(((0, 16.0), (1, 1.0), (2, 16.0), (3, 1.0), (0, 1.0), (4, -128.0), (1, 1.0))):
+        ts(col("CT", j), PM, float(f), Op.is_equal, w, Op.mult)
+    tt(WY, col("CT", 0), col("CT", 1), Op.add)
+    tt(WN, col("CT", 2), col("CT", 3), Op.add)
+    tt(WQ, col("CT", 4), col("CT", 5), Op.add)
+    for j, w in enumerate((WN, col("CT", 6), WQ)):
+        ts(col("CT", 8 + j), w, 1.0 / 1024, Op.mult)
+    ts(K64, PM, 64.0, Op.mult)
+    for r in range(16):
+        ts(R("SU", 128 * r, 128 * r + 128), R("BD"), float(r), Op.is_equal, 1024.0, Op.mult)
+    act_scale(R("SN"), R("SU"), col("CT", 8))
+    fill(R("TF"), 0.0)
+    ts(R("CW", 256, 384), R("NXC"), 4, Op.logical_shift_right)
+    ts(R("CW", 384, 512), R("NXC"), 15, Op.bitwise_and)
+    ts(R("ICm"), R("IC"), P - 1, Op.bitwise_and)
+    ts(R("CW", 0, 128), R("ICm"), 4, Op.logical_shift_right)
+    ts(R("CW", 128, 256), R("ICm"), 15, Op.bitwise_and)
+    cp(R("CF"), R("CW"))
+    for f in range(5):
+        src = R("CF", 128 * f, 128 * f + 128) if f < 4 else R("ONE")
+        dst = R("TF", 0, P, 1, slice(f, 128, 16))
+        dma("S", ap(dst), ap(src), [src], [dst])
+    cp(R("K0"), R("KI"))
+    for k in range(16):
+        cp(R("HX", k, NX * 16, 16), R("H0", 0, NX))
+    ts(R("THw", 0, 2, 1, e8), R("TH", 0, 2, 1, e8), 4032, Op.bitwise_and)
+    ts(R("THw", 2, 4, 1, e8), R("TH", 0, 2, 1, e8), 63, Op.bitwise_and)
+    cp(R("THf", 0, 4, 1, e8), R("THw", 0, 4, 1, e8))
+    for j in range(2):
+        mm(R("p7", 200, 202), R("TSR", p=e8), R("THf", 2 * j, 2 * j + 2, 1, e8), j == 0, j == 1)
+    for s in range(2):
+        for j in range(2):
+            mm(R("p7", 202 + s, 203 + s), R("TS%d" % s, p=e8), R("THf", 2 * j, 2 * j + 1, 1, e8), j == 0, j == 1)
+    ts(R("KBM"), R("ID"), K64, Op.mult)
+    ts(R("NI"), R("ID"), -1.0, Op.mult)
+
+    def more_constants():
+        fill(R("RS0"), BIG)
+        asel(R("RST"), R("RS0"), [[0, 24], [1, 16]], Op.is_equal, -BIG, 0, 0)
+        fill(R("TX", VO, TW), 1024.0)
+        fill(R("BMR"), 0.0)
+        ts(R("BMw", 0, 12), R("BMC"), 4, Op.logical_shift_right)
+        ts(R("BMw", 12, 24), R("BMC"), 15, Op.bitwise_and)
+        cp(R("BMf"), R("BMw"))
+        for f in range(2):
+            src, dst = R("BMf", 12 * f, 12 * f + 12), R("BMR", 0, L, 1, slice(f, 128, 16))
+            dma("S", ap(dst), ap(src), [src], [dst])
+        ts(RM1, R("IW", 1, 2), 16.0, Op.is_ge)
+        ts(RM0, R("IW", 1, 2), 16.0, Op.is_lt)
+        ts(W140, PM, 2.0, Op.is_equal, float(VO // 16), Op.mult)
+        ts(R("TF", HS, VO), R("ON2"), W140, Op.mult)
+        ts(R("CI"), R("I12"), PM, Op.add)
+        for w, wt in enumerate((1.0, 64.0, 4096.0)):
+            for u in range(2):
+                for s in range(2):
+                    m = "ID" if u == s else ("SP" if s else "SM")
+                    j = 4 * w + 2 * u + s
+                    ts(R("PP", 128 * j, 128 * j + 128), R(m), RM1 if u else RM0, Op.mult, wt, Op.mult)
+        cp(R("T2"), R("p7", 200, 202))
+        ts(R("T1K"), R("p7", 202, 204), 1024.0, Op.mult)
+        cp(R("THR"), R("T1K"))
+        ts(R("BO"), R("BD"), 0.0, Op.is_ge)
+        act_scale(R("SR"), R("SU"), col("CT", 9))
+        act_scale(R("SQ"), R("SU"), col("CT", 10))
+
+    def late_constants():
+        ts(R("JL"), R("IL"), PM, Op.add)
+        lists(R("p2", 0), "SN", "TF", 128)
+        cp(R("NL"), R("p2", 0, 128))
+        tt(DJ, R("NL"), R("JL"), Op.subtract)
+        ts(R("RC"), R("R16"), PM, Op.is_equal, 1024.0, Op.mult)
+        for r in range(16):
+            ts(R("MT", 128 * r, 128 * r + 128), R("BO"), col("RC", r), Op.mult)
+        ts(R("N32"), R("N3b"), -1.0, Op.mult)
+        ts(R("WYR"), R("BO"), WY, Op.mult)
+        ts(R("WNR"), R("BO"), WN, Op.mult)
+
+    def bookmarks():
+        agather(R("FB"), R("TF", 0, P), R("BU"))
+        lists(R("p6", 100), "SY", "FB", 12)
+        lists(R("p6", 112), "SN", "FB", 12)
+
+    def bookmark_lists():
+        act(R("JB", 0, 12), R("p6", 100, 112))
+        act_lin(R("JB", 12, 24), R("p6", 112, 124), 1.0, -float(VO))
+
+    def threshold():
+        cp(R("AI"), R("p6", 200, 202))
+        ts(R("AJ"), R("AI"), 31, Op.bitwise_and)
+        ts(R("AK"), R("AJ"), 1024.0, Op.mult)
+        tt(R("THR"), R("AK"), R("T1K"), Op.add)
+
+    for t in range(NV):
+        last = t == NV - 1
+        H, K = "H%d" % t, "K%d" % t
+        if t:
+            cnt = len(topo.engines(prv, core))
+            arrive(H, "ha%d" % t, cnt)
+            arrive(K, "ka%d" % t, cnt)
+            for k in range(GK):
+                asel(R("HX", k, NX * 16, 16), R(H, 0, NX), [[0, NX]], Op.is_ge, 0.0, 1, 0)
+            for k in range(GK, 16):
+                cp(R("HX", k, NX * 16, 16), R(H, 0, NX))
+        agather(R("GB"), R("TX", 0, P), R(K, NX, L))
+        nc = len(CHUNKS) - 1
+        for c in range(nc):
+            a, b = CHUNKS[c], CHUNKS[c + 1]
+            ttgather(R("DX", 16 * a, 16 * b), R("TX", 0, P), R(K, a, b), R("HX", 16 * a, 16 * b), Op.subtract)
+
+        def sums(i0, i1, src):
+            o = R("p0", i0, i1)
+            mm(o, R("KBM"), R("ON2", 0, i1 - i0), True, False)
+            for k in range(16):
+                mm(o, R("SU", 128 * k, 128 * k + 128), src(k), False, k == 15)
+
+        def sums_c(c):
+            a, b = CHUNKS[c], CHUNKS[c + 1]
+            act(R("AX", 16 * a, 16 * b), R("DX", 16 * a, 16 * b), Act.Abs)
+            sums(a, b, lambda k: R("AX", 16 * a + k, 16 * b, 16))
+
+        for k in range(16):
+            o = R("p%d" % (1 + k // 8), (k % 8) * CB, (k % 8) * CB + CB)
+            mm(o, R("ID"), R("GB", k, 16 * CB, 16), True, False)
+            mm(o, R("NI"), R(H, NX, L), False, True)
+        sums_c(0)
+        for j in range(2):
+            act(R("AB", 8 * CB * j, 8 * CB * j + 8 * CB), R("p%d" % (1 + j), 0, 8 * CB), Act.Abs)
+        sums(NX, L, lambda k: R("AB", CB * k, CB * k + CB))
+        for c in range(1, nc):
+            sums_c(c)
+        act(R("TX", HS, VO), R(H))
+        if t:
+            cp(R("KI"), R(K))
+        ts(R("KA", 0, L), R("KI"), 63, Op.bitwise_and)
+        ts(R("KA", L, 2 * L), R("KI"), 6, Op.logical_shift_right)
+        if t:
+            threshold()
+            bookmarks()
+            act(R("JL"), R("p7", 0, 128))
+            bookmark_lists()
+        else:
+            more_constants()
+        tt(R("KAB", 0, L), R("p0", 0, L), R("KA", 0, L), Op.add)
+        tt(R("KAB", L, 2 * L), R("p0", 0, L), R("KA", L, 2 * L), Op.add)
+        op("V", lambda e: e.transpose(ap(R("VT")), ap(R("KAB"))), [R("KAB")], [R("VT")])
+        op("V", lambda e: e.tensor_tensor_scan(ap(R("MS")), ap(R("RST")), ap(R("VT")), BIG, Op.max, Op.min), [R("RST"), R("VT")], [R("MS")])
+        cp(R("MI"), R("MS", 15, 2 * L, 16))
+        for s in range(2):
+            ts(R("MV", s, 12, 2), R("MS", 15 + 16 * s, L, 32), col("THR", s), Op.is_ge)
+        ts(R("ML"), R("MI"), 63, Op.bitwise_and)
+        cp(R("LB"), R("ML"))
+        for u in range(2):
+            for w in (2, 0, 1):
+                for s in range(2):
+                    j = 4 * w + 2 * u + s
+                    src = R("MV", s, 12, 2) if w == 2 else R("LB", 12 * w + s, 12 * w + 12, 2)
+                    mm(R("p3", u, 12, 2), R("PP", 128 * j, 128 * j + 128), src, w == 2 and s == 0, w == 1 and s == 1)
+        tt(R("L1f"), R("p3", 0, 12), R("CI"), Op.min)
+        cp(R("L1"), R("L1f"))
+        ttgather(R("SI"), R("TX", 0, VO), R("L1"), R(H), Op.add)
+        agather(R("FY"), R("TF", 0, VO), R("L1"))
+        ts(R("Q1"), R("SI"), 1, Op.arith_shift_right)
+        ts(R("MISS"), R("p3", 0, 12), 4096.0, Op.is_ge)
+        lists(R("p3", 16), "SN", "FY", 12)
+        if t:
+            tt(DJ, R("NL"), R("JL"), Op.subtract)
+        cp(R("M1"), R("p3", 16, 28))
+        ttgather(R("E2"), R("TX"), R("M1"), R("Q1"), Op.subtract)
+        agather(R("FN"), R("TF"), R("M1"))
+        act(R("AE"), R("E2"), Act.Abs)
+        mm(R("p1", 0, L), R("ID"), R("FN"), True, False)
+        mm(R("p1", 0, L), R("NI"), R("FY"), False, True)
+        mm(R("p5", 0, L), R("BO"), R("AE"))
+        lists2("p4", 0, "SQ", 24)
+        lists2("p3", 40, "SR", 24)
+        ts(R("F2"), R("E2"), 0.5, Op.mult, -0.25, Op.add)
+        ts(R("BR"), R("p5", 0, L), col("T2", 1), Op.is_le)
+        lists(R("p7", 0), "SU", "BR", 12)
+        tt(R("GF"), R("p1", 0, L), R("BR"), Op.mult)
+        if t == 0:
+            for r in range(16):
+                ts(R("SY", 128 * r, 128 * r + 128), R("BD"), float(r), Op.is_equal, WY, Op.mult)
+        if not last:
+            lists2("p5", 256, "SY", 36)
+        tt(R("p2", 0, L), R("F2"), R("BR"), Op.mult)
+        tt(R("HS%d" % t), R("p2", 0, L), R("Q1"), Op.add)
+        if not last:
+            deps("G", [R("HS%d" % t)], [])
+            g.remote_dma(ap(R("H%d" % (t + 1))), ap(R("HS%d" % t)), T.sem["ha%d" % (t + 1)], T.sem["loc"], pid, rid, mask)
+        else:
+            dma("S", T["yh"][:, :], ap(R("HS%d" % t)), [R("HS%d" % t)], [])
+        if t == 0:
+            lists(R("p6", 0), "SY", "BMR", 12)
+        act_lin(R("QR", 0, 24), R("p4", 0, 24), -1.0, 0.5)
+        cp(R("QR", 24, 48), R("p3", 40, 64))
+        for j in range(24):
+            if j == 12:
+                cp(R("BRL"), R("p7", 0, 12))
+            if j < NA:
+                act_bias(R("OQ", QW * j, QW * j + 129), R("IQ"), Act.Sign, col("QR", j))
+            else:
+                ts(R("OQ", QW * j, QW * j + 129), R("IQ"), col("QR", j), Op.add, 0.0, Op.is_gt)
+            if j < 12:
+                ts(R("OR", 128 * j, 128 * j + 128), R("BD"), col("QR", 24 + j), Op.is_equal)
+            else:
+                ts(R("OR", 128 * j, 128 * j + 128), R("BD"), col("QR", 24 + j), Op.is_equal, col("BRL", j - 12), Op.mult)
+        if not last:
+            if t == 0:
+                cp(R("BU"), R("p6", 0, 12))
+                bookmarks()
+                bookmark_lists()
+                late_constants()
+            tt(R("YM", 0, 12), R("JB", 0, 12), R("MISS"), Op.mult)
+            tt(R("YM", 12, 24), R("JB", 12, 24), R("MISS"), Op.mult)
+            tt(R("BY"), R("p5", 256, 268), R("YM", 0, 12), Op.add)
+            tt(R("BN"), R("p3", 16, 28), R("YM", 12, 24), Op.add)
+            tt(R("YF"), R("p5", 280, 292), R("BY"), Op.add)
+            cp(R("YU"), R("YF"))
+            vgather(R("KS%d" % t), R("PL"), R("YU"))
+            deps("G", [R("KS%d" % t)], [])
+            g.remote_dma(ap(R("K%d" % (t + 1))), ap(R("KS%d" % t)), T.sem["ka%d" % (t + 1)], T.sem["loc"], pid, rid, mask)
+        if t == 0:
+            act(R("BB"), R("TF", 0, P))
+        for k, j in enumerate(ORDER):
+            mm(R("p0", 0, 129), R("OR", 128 * j, 128 * j + 128), R("OQ", QW * j, QW * j + 129), k == 0, k == 23)
+        if not last:
+            lists(R("p5", 300), "SN", "GF", 12)
+        cp(R("CS"), R("p0", 0, 128))
+        tt(R("MK"), R("p0", 1, 129), R("CS"), Op.is_gt)
+        tt(R("p2", 0, 128), R("MK"), DJ, Op.mult)
+        tt(R("ZF"), R("p2", 0, 128), R("JL"), Op.add)
+        cp(R("ZU"), R("ZF"))
+        vgather(R("B1", 0, 1024), R("BB"), R("ZU", 0, 64))
+        agather(R("B1", 1024, 2048), R("BB"), R("ZU", 64, 128))
+        if last:
+            mm(R("p5", 0, L), R("WNR"), R("FY"), True, False)
+            mm(R("p5", 0, L), R("WNR"), R("GF"), False, True)
+            mm(R("p6", 0, L), R("WNR"), R("FB"))
+            cp(R("RB", 0, L), R("p5", 0, L))
+            tt(R("RB", L, 2 * L), R("p6", 0, L), R("RB", 0, L), Op.subtract)
+            ts(R("RB", 2 * L, 3 * L), R("RB", 0, L), float(P), Op.is_ge)
+        vgather(R("TF", 0, 1024), R("B1"), R("ZU", 0, 64))
+        agather(R("TF", 1024, 2048), R("B1"), R("ZU", 64, 128))
+        if last:
+            tt(R("RB", 3 * L, 4 * L), R("RB", L, 2 * L), R("RB", 2 * L, 3 * L), Op.mult)
+            tt(R("RB", L, 2 * L), R("RB", 3 * L, 4 * L), R("RB", 0, L), Op.add)
+            src = R("RB", L, 2 * L, 1, slice(0, 128, 16))
+            dma("S", T["yb"][:, :], ap(src), [src], [])
+            for j in range(4):
+                mm(R("p%d" % (1 + j), 0, 512), R("WYR"), R("TF", 512 * j, 512 * j + 512))
+                if j % 2:
+                    act(R("ROW", 512 * j, 512 * j + 512), R("p%d" % (1 + j)))
+                else:
+                    cp(R("ROW", 512 * j, 512 * j + 512), R("p%d" % (1 + j)))
+            src = R("ROW", 0, P, 1, slice(0, 128, 16))
+            dma("S", T["yj"][:, :], ap(src), [src], [])
+            break
+        for j in range(4):
+            b = "p%d" % (1 + j)
+            if j >= 2:
+                mm(R(b), R("ID"), R("XV", 512 * j, 512 * j + 512), True, False)
+            for r in range(16):
+                mm(R(b, r, 512, 16), R("MT", 128 * r, 128 * r + 128), R("MK", 32 * j, 32 * j + 32), j < 2, j < 2 or r == 15)
+        lists(R("p7", 0), "SY", "TF", 128)
+        for j in range(2):
+            tt(R("XV", 512 * j, 512 * j + 512), R("XV", 512 * j, 512 * j + 512), R("p%d" % (1 + j)), Op.add)
+        tt(R("BF"), R("p5", 300, 312), R("BN"), Op.add)
+        cp(R("BU"), R("BF"))
+        for j in (2, 3):
+            act(R("XV", 512 * j, 512 * j + 512), R("p%d" % (1 + j)))
+        cp(R("JU"), R("p7", 0, 128))
+        vgather(R("TX", 0, 1024), R("XV"), R("JU", 0, 64))
+        agather(R("TX", 1024, 2048), R("XV"), R("JU", 64, 128))
+        for b in range(6):
+            mm(R("p6", 200, 202), R("N32"), R("MV", 2 * b, 2 * b + 2), b == 0, b == 5)
+    finish()
+    g.wait_ge(T.sem["loc"], 2 * (NV - 1) * len(topo.engines(core, nxt)))

@@ -1,16 +1,18 @@
 from concourse.mybir import AluOpType as Op, ActivationFunctionType as Act
 
 BIG = 1.0e9
+VOID = 640.0
 L, P, NV = 192, 2048, 5
 HS = P
 VO = P + L
 TW = VO + 16
-NX = 144
+NX = 136
 CB = L - NX
-CHUNKS = (0, 48, 104, 144)
+CHUNKS = (0, 40, 88, 136)
 QW = 130
-NA = 20
-ORDER = list(range(12)) + list(range(NA, 24)) + list(range(12, NA))
+NQ = 5
+LAST1 = 60
+SPLIT = (48, 64, 60)
 GK = 9
 
 B16, F32, I32, U16 = "bfloat16", "float32", "int32", "uint16"
@@ -22,11 +24,12 @@ SCRATCH = {
     "KI": ("sbuf", [128, L], I32), "KA": ("sbuf", [128, 2 * L], I32), "KAB": ("sbuf", [128, 2 * L], F32),
     "VT": ("sbuf", [128, 2 * L], F32), "MS": ("sbuf", [128, 2 * L], F32), "RST": ("sbuf", [128, 2 * L], F32), "RS0": ("sbuf", [128, 2 * L], F32),
     "MI": ("sbuf", [128, 24], I32), "ML": ("sbuf", [128, 24], I32), "LB": ("sbuf", [128, 24], B16), "MV": ("sbuf", [128, 12], B16),
-    "L1f": ("sbuf", [128, 12], F32), "L1": ("sbuf", [128, 12], U16), "MISS": ("sbuf", [128, 12], F32), "CI": ("sbuf", [128, 12], F32),
+    "L1": ("sbuf", [128, 12], U16), "MISS": ("sbuf", [128, 12], F32), "CV": ("sbuf", [128, 24], F32), "SEL": ("sbuf", [128, 24], F32),
+    "IV": ("sbuf", [128, 12], I32), "IX": ("sbuf", [128, 24], I32),
     "SI": ("sbuf", [128, L], I32), "Q1": ("sbuf", [128, L], I32), "FF": ("sbuf", [128, 3 * L], B16),
     "M1": ("sbuf", [128, 12], U16), "E2": ("sbuf", [128, L], B16), "AE": ("sbuf", [128, L], B16), "F2": ("sbuf", [128, L], I32),
     "BR": ("sbuf", [128, L], B16), "QR": ("sbuf", [128, 48], F32), "BRL": ("sbuf", [128, 12], F32),
-    "BY": ("sbuf", [128, 12], F32), "BN": ("sbuf", [128, 12], F32), "YM": ("sbuf", [128, 24], F32),
+    "BN": ("sbuf", [128, 12], F32), "YM": ("sbuf", [128, 24], F32),
     "YF": ("sbuf", [128, 12], F32), "YU": ("sbuf", [128, 12], U16), "BF": ("sbuf", [128, 12], F32), "BU": ("sbuf", [128, 12], U16),
     "JB": ("sbuf", [128, 24], F32), "FB": ("sbuf", [128, L], B16),
     "OR": ("sbuf", [128, 24 * 128], B16), "OQ": ("sbuf", [128, 24 * QW], B16), "CS": ("sbuf", [128, 128], F32),
@@ -35,12 +38,12 @@ SCRATCH = {
     "AI": ("sbuf", [128, 2], I32), "AJ": ("sbuf", [128, 2], I32), "AK": ("sbuf", [128, 2], F32), "THR": ("sbuf", [128, 2], F32),
     "T1K": ("sbuf", [128, 2], F32), "T2": ("sbuf", [128, 2], F32),
     "ROW": ("sbuf", [128, P], F32), "RB": ("sbuf", [128, 4 * L], F32),
-    "BD": ("sbuf", [128, 128], B16), "ONE": ("sbuf", [128, 128], B16), "ON2": ("sbuf", [128, L], B16),
+    "BD": ("sbuf", [128, 128], B16), "ONE": ("sbuf", [128, 128], B16), "ZER": ("sbuf", [128, 128], B16), "ON2": ("sbuf", [128, L], B16),
     "ID": ("sbuf", [128, 128], B16), "NI": ("sbuf", [128, 128], B16), "SP": ("sbuf", [128, 128], B16), "SM": ("sbuf", [128, 128], B16),
     "N32": ("sbuf", [128, 128], B16), "KBM": ("sbuf", [128, 128], B16), "BO": ("sbuf", [128, 128], B16),
     "WYR": ("sbuf", [128, 128], B16), "WNR": ("sbuf", [128, 128], B16), "IQ": ("sbuf", [128, 129], B16),
     "SU": ("sbuf", [128, 2048], B16), "SY": ("sbuf", [128, 2048], B16), "SN": ("sbuf", [128, 2048], B16), "SQ": ("sbuf", [128, 2048], B16),
-    "SR": ("sbuf", [128, 2048], B16), "MT": ("sbuf", [128, 2048], B16), "PP": ("sbuf", [128, 12 * 128], B16),
+    "SR": ("sbuf", [128, 2048], B16), "MT": ("sbuf", [128, 2048], B16), "PP": ("sbuf", [128, 8 * 128], B16),
     "CO": ("sbuf", [128, 16], F32), "CT": ("sbuf", [128, 16], F32), "RC": ("sbuf", [128, 16], F32), "R16": ("sbuf", [128, 16], F32),
     "IP": ("sbuf", [128, 2], I32), "IW": ("sbuf", [128, 2], I32), "IL": ("sbuf", [128, 128], I32), "I12": ("sbuf", [128, 12], I32), "IC": ("sbuf", [128, 128], I32),
     "CF": ("sbuf", [128, 4 * 128], B16), "CW": ("sbuf", [128, 4 * 128], I32), "NXC": ("sbuf", [128, 128], I32), "ICm": ("sbuf", [128, 128], I32),
@@ -62,7 +65,7 @@ for _k, _n in enumerate(("FY", "FN", "GF")):
     ALIAS[_n] = ("FF", L * _k, L)
 for _t in range(8):
     SCRATCH["p%d" % _t] = ("psum", [128, 512], F32)
-NDMA = 24
+NDMA = 32
 SEMAPHORES = ["sV", "sA", "sT", "sG", "loc"] + ["d%d" % k for k in range(NDMA)] + ["ha%d" % t for t in range(1, NV)] + ["ka%d" % t for t in range(1, NV)]
 
 
@@ -242,13 +245,14 @@ def rank_program(g, core, T, topo):
 
     fill(R("ONE"), 1.0)
     fill(R("ON2"), 1.0)
+    fill(R("ZER"), 0.0)
     iota(R("IP"), [[0, 2]], 0, 1)
     iota(R("BD0"), [[0, 8], [1, 16]], 0, 0)
     asel(R("BD1"), R("BD0"), [[-16, 8], [0, 16]], Op.is_ge, -1.0, 0, 1)
     asel(R("BD"), R("BD1"), [[16, 8], [0, 16]], Op.is_ge, -1.0, 15, -1)
     asel(R("ID"), R("ONE"), [[-1, 128]], Op.is_equal, 0.0, 0, 1)
     iota(R("IC"), [[1, 128]], 0, 128)
-    iota(R("I12"), [[16, 12]], P, 0)
+    iota(R("I12"), [[32, 6], [0, 2]], 0, 0)
     asel(R("SP"), R("ONE"), [[-1, 128]], Op.is_equal, 0.0, 16, 1)
     asel(R("SM"), R("ONE"), [[-1, 128]], Op.is_equal, 0.0, -16, 1)
     e8 = slice(0, 8)
@@ -263,7 +267,7 @@ def rank_program(g, core, T, topo):
     asel(R("N3b"), R("N3a"), [[32, 4], [0, 32]], Op.is_ge, 0.0, 31, -1)
 
     PM, RM1, RM0 = col("CO", 0), col("CO", 1), col("CO", 2)
-    WY, WN, WQ, WR, K64, W140 = (col("CO", j) for j in range(3, 9))
+    WY, WN, WQ, K64, W140, P32 = (col("CO", j) for j in range(3, 9))
     ts(R("IW", 0, 1), R("IP", 0, 1), 15, Op.bitwise_and)
     ts(R("IW", 1, 2), R("IP", 1, 2), 31, Op.bitwise_and)
     cp(PM, R("IW", 0, 1))
@@ -278,15 +282,15 @@ def rank_program(g, core, T, topo):
     for r in range(16):
         ts(R("SU", 128 * r, 128 * r + 128), R("BD"), float(r), Op.is_equal, 1024.0, Op.mult)
     act_scale(R("SN"), R("SU"), col("CT", 8))
-    fill(R("TF"), 0.0)
+    act_scale(R("SR"), R("SU"), col("CT", 9))
     ts(R("CW", 256, 384), R("NXC"), 4, Op.logical_shift_right)
     ts(R("CW", 384, 512), R("NXC"), 15, Op.bitwise_and)
     ts(R("ICm"), R("IC"), P - 1, Op.bitwise_and)
     ts(R("CW", 0, 128), R("ICm"), 4, Op.logical_shift_right)
     ts(R("CW", 128, 256), R("ICm"), 15, Op.bitwise_and)
     cp(R("CF"), R("CW"))
-    for f in range(5):
-        src = R("CF", 128 * f, 128 * f + 128) if f < 4 else R("ONE")
+    for f in range(16):
+        src = R("CF", 128 * f, 128 * f + 128) if f < 4 else R("ONE" if f == 4 else "ZER")
         dst = R("TF", 0, P, 1, slice(f, 128, 16))
         dma("S", ap(dst), ap(src), [src], [dst])
     cp(R("K0"), R("KI"))
@@ -304,22 +308,36 @@ def rank_program(g, core, T, topo):
     ts(R("NI"), R("ID"), -1.0, Op.mult)
 
     def more_constants():
-        fill(R("RS0"), BIG)
+        ts(R("BO"), R("BD"), 0.0, Op.is_ge)
+        cp(P32, R("IW", 1, 2))
+        ts(R("RC"), R("R16"), PM, Op.is_equal, VOID, Op.mult)
+        ts(R("WYR"), R("BO"), WY, Op.mult)
+        ts(R("IV"), R("I12"), P32, Op.add)
+        act_scale(R("SQ"), R("SU"), col("CT", 10))
+        for r in range(16):
+            act_scale(R("MT", 128 * r, 128 * r + 128), R("BO"), col("RC", r))
+        lists(R("p2", 0), "SN", "TF", 128)
+        act(R("NL"), R("p2", 0, 128))
+        fill(R("TF", VO, TW), 0.0)
+        iota(R("RS0"), [[0, 2 * L]], 2 ** 24 - 1, 0)
         asel(R("RST"), R("RS0"), [[0, 24], [1, 16]], Op.is_equal, -BIG, 0, 0)
         fill(R("TX", VO, TW), 1024.0)
         fill(R("BMR"), 0.0)
         ts(R("BMw", 0, 12), R("BMC"), 4, Op.logical_shift_right)
         ts(R("BMw", 12, 24), R("BMC"), 15, Op.bitwise_and)
+        ts(R("IX", 0, 12), R("IV"), 63, Op.bitwise_and)
+        ts(R("IX", 12, 24), R("IV"), 6, Op.logical_shift_right)
+        ts(W140, PM, 2.0, Op.is_equal, float(VO // 16), Op.mult)
         cp(R("BMf"), R("BMw"))
         for f in range(2):
             src, dst = R("BMf", 12 * f, 12 * f + 12), R("BMR", 0, L, 1, slice(f, 128, 16))
             dma("S", ap(dst), ap(src), [src], [dst])
         ts(RM1, R("IW", 1, 2), 16.0, Op.is_ge)
         ts(RM0, R("IW", 1, 2), 16.0, Op.is_lt)
-        ts(W140, PM, 2.0, Op.is_equal, float(VO // 16), Op.mult)
         ts(R("TF", HS, VO), R("ON2"), W140, Op.mult)
-        ts(R("CI"), R("I12"), PM, Op.add)
-        for w, wt in enumerate((1.0, 64.0, 4096.0)):
+        ts(R("CV", 0, 12), R("IX", 0, 12), 64.0, Op.add)
+        ts(R("CV", 12, 24), R("IX", 12, 24), float(HS // 64 - 1), Op.add)
+        for w, wt in enumerate((1.0, 64.0)):
             for u in range(2):
                 for s in range(2):
                     m = "ID" if u == s else ("SP" if s else "SM")
@@ -327,21 +345,15 @@ def rank_program(g, core, T, topo):
                     ts(R("PP", 128 * j, 128 * j + 128), R(m), RM1 if u else RM0, Op.mult, wt, Op.mult)
         cp(R("T2"), R("p7", 200, 202))
         ts(R("T1K"), R("p7", 202, 204), 1024.0, Op.mult)
-        cp(R("THR"), R("T1K"))
-        ts(R("BO"), R("BD"), 0.0, Op.is_ge)
-        act_scale(R("SR"), R("SU"), col("CT", 9))
-        act_scale(R("SQ"), R("SU"), col("CT", 10))
+        ts(R("THR"), R("p7", 202, 204), 1024.0, Op.mult)
+        for r in range(16):
+            asel(R("SY", 128 * r, 128 * r + 128), R("WYR"), [[0, 8], [1, 16]], Op.is_equal, 0.0, -r, 0)
+        dma("S", ap(R("BB")), ap(R("TF", 0, P)), [R("TF", 0, P)], [R("BB")])
 
     def late_constants():
-        ts(R("JL"), R("IL"), PM, Op.add)
-        lists(R("p2", 0), "SN", "TF", 128)
-        cp(R("NL"), R("p2", 0, 128))
-        tt(DJ, R("NL"), R("JL"), Op.subtract)
-        ts(R("RC"), R("R16"), PM, Op.is_equal, 1024.0, Op.mult)
-        for r in range(16):
-            ts(R("MT", 128 * r, 128 * r + 128), R("BO"), col("RC", r), Op.mult)
+        ts(R("JL", 0, 64), R("IL", 0, 64), PM, Op.add)
+        ts(R("JL", 64, 128), R("IL", 64, 128), PM, Op.add)
         ts(R("N32"), R("N3b"), -1.0, Op.mult)
-        ts(R("WYR"), R("BO"), WY, Op.mult)
         ts(R("WNR"), R("BO"), WN, Op.mult)
 
     def bookmarks():
@@ -352,12 +364,6 @@ def rank_program(g, core, T, topo):
     def bookmark_lists():
         act(R("JB", 0, 12), R("p6", 100, 112))
         act_lin(R("JB", 12, 24), R("p6", 112, 124), 1.0, -float(VO))
-
-    def threshold():
-        cp(R("AI"), R("p6", 200, 202))
-        ts(R("AJ"), R("AI"), 31, Op.bitwise_and)
-        ts(R("AK"), R("AJ"), 1024.0, Op.mult)
-        tt(R("THR"), R("AK"), R("T1K"), Op.add)
 
     for t in range(NV):
         last = t == NV - 1
@@ -370,22 +376,28 @@ def rank_program(g, core, T, topo):
                 asel(R("HX", k, NX * 16, 16), R(H, 0, NX), [[0, NX]], Op.is_ge, 0.0, 1, 0)
             for k in range(GK, 16):
                 cp(R("HX", k, NX * 16, 16), R(H, 0, NX))
+            cp(R("KI"), R(K))
         agather(R("GB"), R("TX", 0, P), R(K, NX, L))
         nc = len(CHUNKS) - 1
         for c in range(nc):
             a, b = CHUNKS[c], CHUNKS[c + 1]
             ttgather(R("DX", 16 * a, 16 * b), R("TX", 0, P), R(K, a, b), R("HX", 16 * a, 16 * b), Op.subtract)
 
-        def sums(i0, i1, src):
+        def sums(i0, i1, *srcs):
             o = R("p0", i0, i1)
             mm(o, R("KBM"), R("ON2", 0, i1 - i0), True, False)
-            for k in range(16):
-                mm(o, R("SU", 128 * k, 128 * k + 128), src(k), False, k == 15)
+            for src in srcs:
+                for k in range(16):
+                    mm(o, R("SU", 128 * k, 128 * k + 128), src(k), False, k == 15 and src is srcs[-1])
 
         def sums_c(c):
             a, b = CHUNKS[c], CHUNKS[c + 1]
-            act(R("AX", 16 * a, 16 * b), R("DX", 16 * a, 16 * b), Act.Abs)
-            sums(a, b, lambda k: R("AX", 16 * a + k, 16 * b, 16))
+            if c == nc - 1:
+                ts(R("AX", 16 * a, 16 * b), R("DX", 16 * a, 16 * b), -2.0, Op.mult, 0.0, Op.max)
+                sums(a, b, lambda k: R("DX", 16 * a + k, 16 * b, 16), lambda k: R("AX", 16 * a + k, 16 * b, 16))
+            else:
+                act(R("AX", 16 * a, 16 * b), R("DX", 16 * a, 16 * b), Act.Abs)
+                sums(a, b, lambda k: R("AX", 16 * a + k, 16 * b, 16))
 
         for k in range(16):
             o = R("p%d" % (1 + k // 8), (k % 8) * CB, (k % 8) * CB + CB)
@@ -399,13 +411,17 @@ def rank_program(g, core, T, topo):
             sums_c(c)
         act(R("TX", HS, VO), R(H))
         if t:
-            cp(R("KI"), R(K))
+            cp(R("AI"), R("p6", 200, 202))
         ts(R("KA", 0, L), R("KI"), 63, Op.bitwise_and)
+        if t:
+            ts(R("AJ"), R("AI"), 31, Op.bitwise_and)
         ts(R("KA", L, 2 * L), R("KI"), 6, Op.logical_shift_right)
         if t:
-            threshold()
+            ts(R("AK"), R("AJ"), 1024.0, Op.mult)
+            tt(R("THR"), R("AK"), R("T1K"), Op.add)
             bookmarks()
-            act(R("JL"), R("p7", 0, 128))
+            act(R("JL", SPLIT[2], 128), R("p7", SPLIT[2], 128))
+            act(R("JL", 0, SPLIT[2]), R("p5", 0, SPLIT[2]))
             bookmark_lists()
         else:
             more_constants()
@@ -417,22 +433,30 @@ def rank_program(g, core, T, topo):
         for s in range(2):
             ts(R("MV", s, 12, 2), R("MS", 15 + 16 * s, L, 32), col("THR", s), Op.is_ge)
         ts(R("ML"), R("MI"), 63, Op.bitwise_and)
-        cp(R("LB"), R("ML"))
+        for w in range(2):
+            tt(R("SEL", 12 * w, 12 * w + 12), R("MV"), R("CV", 12 * w, 12 * w + 12), Op.mult)
+        tt(R("LB"), R("ML"), R("SEL"), Op.max)
         for u in range(2):
-            for w in (2, 0, 1):
+            for w in range(2):
                 for s in range(2):
                     j = 4 * w + 2 * u + s
-                    src = R("MV", s, 12, 2) if w == 2 else R("LB", 12 * w + s, 12 * w + 12, 2)
-                    mm(R("p3", u, 12, 2), R("PP", 128 * j, 128 * j + 128), src, w == 2 and s == 0, w == 1 and s == 1)
-        tt(R("L1f"), R("p3", 0, 12), R("CI"), Op.min)
-        cp(R("L1"), R("L1f"))
+                    mm(R("p3", u, 12, 2), R("PP", 128 * j, 128 * j + 128), R("LB", 12 * w + s, 12 * w + 12, 2), w == 0 and s == 0, w == 1 and s == 1)
+        cp(R("L1"), R("p3", 0, 12))
+
+        def missed():
+            tt(R("YM", 0, 12), R("JB", 0, 12), R("MISS"), Op.mult)
+            tt(R("YM", 12, 24), R("JB", 12, 24), R("MISS"), Op.mult)
+
         ttgather(R("SI"), R("TX", 0, VO), R("L1"), R(H), Op.add)
         agather(R("FY"), R("TF", 0, VO), R("L1"))
+        ts(R("MISS"), R("p3", 0, 12), float(HS), Op.is_ge)
         ts(R("Q1"), R("SI"), 1, Op.arith_shift_right)
-        ts(R("MISS"), R("p3", 0, 12), 4096.0, Op.is_ge)
+        if t and not last:
+            missed()
         lists(R("p3", 16), "SN", "FY", 12)
-        if t:
-            tt(DJ, R("NL"), R("JL"), Op.subtract)
+        if t == 0:
+            late_constants()
+        tt(DJ, R("NL"), R("JL"), Op.subtract)
         cp(R("M1"), R("p3", 16, 28))
         ttgather(R("E2"), R("TX"), R("M1"), R("Q1"), Op.subtract)
         agather(R("FN"), R("TF"), R("M1"))
@@ -445,13 +469,8 @@ def rank_program(g, core, T, topo):
         ts(R("F2"), R("E2"), 0.5, Op.mult, -0.25, Op.add)
         ts(R("BR"), R("p5", 0, L), col("T2", 1), Op.is_le)
         lists(R("p7", 0), "SU", "BR", 12)
-        tt(R("GF"), R("p1", 0, L), R("BR"), Op.mult)
-        if t == 0:
-            for r in range(16):
-                ts(R("SY", 128 * r, 128 * r + 128), R("BD"), float(r), Op.is_equal, WY, Op.mult)
-        if not last:
-            lists2("p5", 256, "SY", 36)
         tt(R("p2", 0, L), R("F2"), R("BR"), Op.mult)
+        cp(R("QR", 24, 48), R("p3", 40, 64))
         tt(R("HS%d" % t), R("p2", 0, L), R("Q1"), Op.add)
         if not last:
             deps("G", [R("HS%d" % t)], [])
@@ -461,11 +480,10 @@ def rank_program(g, core, T, topo):
         if t == 0:
             lists(R("p6", 0), "SY", "BMR", 12)
         act_lin(R("QR", 0, 24), R("p4", 0, 24), -1.0, 0.5)
-        cp(R("QR", 24, 48), R("p3", 40, 64))
         for j in range(24):
-            if j == 12:
+            if j == 10:
                 cp(R("BRL"), R("p7", 0, 12))
-            if j < NA:
+            if j >= NQ:
                 act_bias(R("OQ", QW * j, QW * j + 129), R("IQ"), Act.Sign, col("QR", j))
             else:
                 ts(R("OQ", QW * j, QW * j + 129), R("IQ"), col("QR", j), Op.add, 0.0, Op.is_gt)
@@ -473,34 +491,41 @@ def rank_program(g, core, T, topo):
                 ts(R("OR", 128 * j, 128 * j + 128), R("BD"), col("QR", 24 + j), Op.is_equal)
             else:
                 ts(R("OR", 128 * j, 128 * j + 128), R("BD"), col("QR", 24 + j), Op.is_equal, col("BRL", j - 12), Op.mult)
+        tt(R("GF"), R("p1", 0, L), R("BR"), Op.mult)
+        if t == 0:
+            cp(R("BU"), R("p6", 0, 12))
         if not last:
+            for r in range(16):
+                mm(R("p5", 256, 268), R("SY", 128 * r, 128 * r + 128), R("FY", r, L, 16), r == 0, False)
+        for j in range(24):
+            mm(R("p0", 0, 129), R("OR", 128 * j, 128 * j + 128), R("OQ", QW * j, QW * j + 129), j == 0, j == 23)
+        if not last:
+            for r in range(16):
+                mm(R("p5", 256, 268), R("SY", 128 * r, 128 * r + 128), R("GF", r, L, 16), False, r == 15)
+            lists(R("p4", 100), "SN", "GF", 12)
             if t == 0:
-                cp(R("BU"), R("p6", 0, 12))
                 bookmarks()
                 bookmark_lists()
-                late_constants()
-            tt(R("YM", 0, 12), R("JB", 0, 12), R("MISS"), Op.mult)
-            tt(R("YM", 12, 24), R("JB", 12, 24), R("MISS"), Op.mult)
-            tt(R("BY"), R("p5", 256, 268), R("YM", 0, 12), Op.add)
-            tt(R("BN"), R("p3", 16, 28), R("YM", 12, 24), Op.add)
-            tt(R("YF"), R("p5", 280, 292), R("BY"), Op.add)
-            cp(R("YU"), R("YF"))
-            vgather(R("KS%d" % t), R("PL"), R("YU"))
-            deps("G", [R("KS%d" % t)], [])
-            g.remote_dma(ap(R("K%d" % (t + 1))), ap(R("KS%d" % t)), T.sem["ka%d" % (t + 1)], T.sem["loc"], pid, rid, mask)
-        if t == 0:
-            act(R("BB"), R("TF", 0, P))
-        for k, j in enumerate(ORDER):
-            mm(R("p0", 0, 129), R("OR", 128 * j, 128 * j + 128), R("OQ", QW * j, QW * j + 129), k == 0, k == 23)
-        if not last:
-            lists(R("p5", 300), "SN", "GF", 12)
         cp(R("CS"), R("p0", 0, 128))
         tt(R("MK"), R("p0", 1, 129), R("CS"), Op.is_gt)
         tt(R("p2", 0, 128), R("MK"), DJ, Op.mult)
         tt(R("ZF"), R("p2", 0, 128), R("JL"), Op.add)
         cp(R("ZU"), R("ZF"))
-        vgather(R("B1", 0, 1024), R("BB"), R("ZU", 0, 64))
-        agather(R("B1", 1024, 2048), R("BB"), R("ZU", 64, 128))
+        s1, s2, s3 = SPLIT
+        if last:
+            s1 = LAST1
+        agather(R("B1", 16 * s1, P), R("BB"), R("ZU", s1, 128))
+        if not last:
+            if t == 0:
+                missed()
+            tt(R("YF"), R("p5", 256, 268), R("YM", 0, 12), Op.add)
+            tt(R("BN"), R("p3", 16, 28), R("YM", 12, 24), Op.add)
+            cp(R("YU"), R("YF"))
+            vgather(R("KS%d" % t), R("PL"), R("YU"))
+            deps("G", [R("KS%d" % t)], [])
+            g.remote_dma(ap(R("K%d" % (t + 1))), ap(R("KS%d" % t)), T.sem["ka%d" % (t + 1)], T.sem["loc"], pid, rid, mask)
+            tt(R("BF"), R("p4", 100, 112), R("BN"), Op.add)
+        vgather(R("B1", 0, 16 * s1), R("BB"), R("ZU", 0, s1))
         if last:
             mm(R("p5", 0, L), R("WNR"), R("FY"), True, False)
             mm(R("p5", 0, L), R("WNR"), R("GF"), False, True)
@@ -508,8 +533,8 @@ def rank_program(g, core, T, topo):
             cp(R("RB", 0, L), R("p5", 0, L))
             tt(R("RB", L, 2 * L), R("p6", 0, L), R("RB", 0, L), Op.subtract)
             ts(R("RB", 2 * L, 3 * L), R("RB", 0, L), float(P), Op.is_ge)
-        vgather(R("TF", 0, 1024), R("B1"), R("ZU", 0, 64))
-        agather(R("TF", 1024, 2048), R("B1"), R("ZU", 64, 128))
+        vgather(R("TF", 0, 16 * s2), R("B1"), R("ZU", 0, s2))
+        agather(R("TF", 16 * s2, P), R("B1"), R("ZU", s2, 128))
         if last:
             tt(R("RB", 3 * L, 4 * L), R("RB", L, 2 * L), R("RB", 2 * L, 3 * L), Op.mult)
             tt(R("RB", L, 2 * L), R("RB", 3 * L, 4 * L), R("RB", 0, L), Op.add)
@@ -530,16 +555,18 @@ def rank_program(g, core, T, topo):
                 mm(R(b), R("ID"), R("XV", 512 * j, 512 * j + 512), True, False)
             for r in range(16):
                 mm(R(b, r, 512, 16), R("MT", 128 * r, 128 * r + 128), R("MK", 32 * j, 32 * j + 32), j < 2, j < 2 or r == 15)
-        lists(R("p7", 0), "SY", "TF", 128)
-        for j in range(2):
-            tt(R("XV", 512 * j, 512 * j + 512), R("XV", 512 * j, 512 * j + 512), R("p%d" % (1 + j)), Op.add)
-        tt(R("BF"), R("p5", 300, 312), R("BN"), Op.add)
-        cp(R("BU"), R("BF"))
+        for b, q0, q1 in (("p7", s3, 128), ("p5", 0, s3)):
+            for r in range(16):
+                mm(R(b, q0, q1), R("SY", 128 * r, 128 * r + 128), R("TF", 16 * q0 + r, 16 * q1, 16), r == 0, r == 15)
         for j in (2, 3):
             act(R("XV", 512 * j, 512 * j + 512), R("p%d" % (1 + j)))
-        cp(R("JU"), R("p7", 0, 128))
-        vgather(R("TX", 0, 1024), R("XV"), R("JU", 0, 64))
-        agather(R("TX", 1024, 2048), R("XV"), R("JU", 64, 128))
+        tt(R("XV", 0, 512), R("XV", 0, 512), R("p1"), Op.add)
+        tt(R("XV", 512, 1024), R("XV", 512, 1024), R("p2"), Op.add)
+        cp(R("JU", s3, 128), R("p7", s3, 128))
+        cp(R("JU", 0, s3), R("p5", 0, s3))
+        cp(R("BU"), R("BF"))
+        vgather(R("TX", 0, 16 * s3), R("XV"), R("JU", 0, s3))
+        agather(R("TX", 16 * s3, P), R("XV"), R("JU", s3, 128))
         for b in range(6):
             mm(R("p6", 200, 202), R("N32"), R("MV", 2 * b, 2 * b + 2), b == 0, b == 5)
     finish()

@@ -6,13 +6,14 @@ L, P, NV = 192, 2048, 5
 HS = P
 VO = P + L
 TW = VO + 16
-NX = 136
+NX = 128
 CB = L - NX
-CHUNKS = (0, 40, 88, 136)
+CHUNKS = (0, 64, 128)
 QW = 130
+PRE = 5
 NQ = 5
 LAST1 = 60
-SPLIT = (48, 64, 60)
+SPLIT = (50, 60, 60)
 GK = 9
 
 B16, F32, I32, U16 = "bfloat16", "float32", "int32", "uint16"
@@ -358,6 +359,9 @@ def rank_program(g, core, T, topo):
 
     def bookmarks():
         agather(R("FB"), R("TF", 0, P), R("BU"))
+        bookmark_fields()
+
+    def bookmark_fields():
         lists(R("p6", 100), "SY", "FB", 12)
         lists(R("p6", 112), "SN", "FB", 12)
 
@@ -369,13 +373,6 @@ def rank_program(g, core, T, topo):
         last = t == NV - 1
         H, K = "H%d" % t, "K%d" % t
         if t:
-            cnt = len(topo.engines(prv, core))
-            arrive(H, "ha%d" % t, cnt)
-            arrive(K, "ka%d" % t, cnt)
-            for k in range(GK):
-                asel(R("HX", k, NX * 16, 16), R(H, 0, NX), [[0, NX]], Op.is_ge, 0.0, 1, 0)
-            for k in range(GK, 16):
-                cp(R("HX", k, NX * 16, 16), R(H, 0, NX))
             cp(R("KI"), R(K))
         agather(R("GB"), R("TX", 0, P), R(K, NX, L))
         nc = len(CHUNKS) - 1
@@ -393,6 +390,8 @@ def rank_program(g, core, T, topo):
         def sums_c(c):
             a, b = CHUNKS[c], CHUNKS[c + 1]
             if c == nc - 1:
+                if t:
+                    cp(R("AI"), R("p6", 200, 202))
                 ts(R("AX", 16 * a, 16 * b), R("DX", 16 * a, 16 * b), -2.0, Op.mult, 0.0, Op.max)
                 sums(a, b, lambda k: R("DX", 16 * a + k, 16 * b, 16), lambda k: R("AX", 16 * a + k, 16 * b, 16))
             else:
@@ -406,12 +405,10 @@ def rank_program(g, core, T, topo):
         sums_c(0)
         for j in range(2):
             act(R("AB", 8 * CB * j, 8 * CB * j + 8 * CB), R("p%d" % (1 + j), 0, 8 * CB), Act.Abs)
-        sums(NX, L, lambda k: R("AB", CB * k, CB * k + CB))
-        for c in range(1, nc):
+        for c in range(nc - 1, 0, -1):
             sums_c(c)
+        sums(NX, L, lambda k: R("AB", CB * k, CB * k + CB))
         act(R("TX", HS, VO), R(H))
-        if t:
-            cp(R("AI"), R("p6", 200, 202))
         ts(R("KA", 0, L), R("KI"), 63, Op.bitwise_and)
         if t:
             ts(R("AJ"), R("AI"), 31, Op.bitwise_and)
@@ -425,17 +422,28 @@ def rank_program(g, core, T, topo):
             bookmark_lists()
         else:
             more_constants()
-        tt(R("KAB", 0, L), R("p0", 0, L), R("KA", 0, L), Op.add)
-        tt(R("KAB", L, 2 * L), R("p0", 0, L), R("KA", L, 2 * L), Op.add)
-        op("V", lambda e: e.transpose(ap(R("VT")), ap(R("KAB"))), [R("KAB")], [R("VT")])
-        op("V", lambda e: e.tensor_tensor_scan(ap(R("MS")), ap(R("RST")), ap(R("VT")), BIG, Op.max, Op.min), [R("RST"), R("VT")], [R("MS")])
-        cp(R("MI"), R("MS", 15, 2 * L, 16))
+        def half(name, w):
+            return R(name, L * w, L * w + L)
+
+        def twelve(name, w):
+            return R(name, 12 * w, 12 * w + 12)
+
+        for w in range(2):
+            tt(half("KAB", w), R("p0", 0, L), half("KA", w), Op.add)
+        for w in range(2):
+            op("V", lambda e: e.transpose(ap(half("VT", w)), ap(half("KAB", w))), [half("KAB", w)], [half("VT", w)])
+        for w in range(2):
+            op("V", lambda e: e.tensor_tensor_scan(ap(half("MS", w)), ap(half("RST", w)), ap(half("VT", w)), BIG, Op.max, Op.min), [half("RST", w), half("VT", w)], [half("MS", w)])
+        cp(twelve("MI", 0), R("MS", 15, L, 16))
         for s in range(2):
             ts(R("MV", s, 12, 2), R("MS", 15 + 16 * s, L, 32), col("THR", s), Op.is_ge)
-        ts(R("ML"), R("MI"), 63, Op.bitwise_and)
+        cp(twelve("MI", 1), R("MS", L + 15, 2 * L, 16))
+        ts(twelve("ML", 0), twelve("MI", 0), 63, Op.bitwise_and)
         for w in range(2):
-            tt(R("SEL", 12 * w, 12 * w + 12), R("MV"), R("CV", 12 * w, 12 * w + 12), Op.mult)
-        tt(R("LB"), R("ML"), R("SEL"), Op.max)
+            tt(twelve("SEL", w), R("MV"), twelve("CV", w), Op.mult)
+        ts(twelve("ML", 1), twelve("MI", 1), 63, Op.bitwise_and)
+        for w in range(2):
+            tt(twelve("LB", w), twelve("ML", w), twelve("SEL", w), Op.max)
         for u in range(2):
             for w in range(2):
                 for s in range(2):
@@ -461,62 +469,90 @@ def rank_program(g, core, T, topo):
         ttgather(R("E2"), R("TX"), R("M1"), R("Q1"), Op.subtract)
         agather(R("FN"), R("TF"), R("M1"))
         act(R("AE"), R("E2"), Act.Abs)
+        def one_hot(j):
+            if j < 12:
+                ts(R("OR", 128 * j, 128 * j + 128), R("BD"), col("QR", 24 + j), Op.is_equal)
+            else:
+                ts(R("OR", 128 * j, 128 * j + 128), R("BD"), col("QR", 24 + j), Op.is_equal, col("BRL", j - 12), Op.mult)
+
+        def steps(j):
+            if j < 24 - NQ:
+                act_bias(R("OQ", QW * j, QW * j + 129), R("IQ"), Act.Sign, col("QR", j))
+            else:
+                ts(R("OQ", QW * j, QW * j + 129), R("IQ"), col("QR", j), Op.add, 0.0, Op.is_gt)
+
+        def products(j0, j1):
+            for j in range(j0, j1):
+                mm(R("p0", 0, 129), R("OR", 128 * j, 128 * j + 128), R("OQ", QW * j, QW * j + 129), j == 0, j == 23)
+
+        lists(R("p6", 140), "SR", "FY", 12)
+        lists(R("p4", 0), "SQ", "FY", 12)
+        mm(R("p5", 0, L), R("BO"), R("AE"))
+        cp(R("QR", 24, 36), R("p6", 140, 152))
+        ts(R("F2"), R("E2"), 0.5, Op.mult, -0.25, Op.add)
+        act_lin(R("QR", 0, 12), R("p4", 0, 12), -1.0, 0.5)
+        for j in range(12):
+            steps(j)
+        for j in range(PRE):
+            one_hot(j)
+        ts(R("BR"), R("p5", 0, L), col("T2", 1), Op.is_le)
+        for j in range(PRE, 12):
+            one_hot(j)
+        lists(R("p4", 12), "SQ", "FN", 12)
+        lists(R("p3", 52), "SR", "FN", 12)
+        lists(R("p7", 0), "SU", "BR", 12)
+        if t == 0:
+            lists(R("p6", 0), "SY", "BMR", 12)
+        products(0, 12)
         mm(R("p1", 0, L), R("ID"), R("FN"), True, False)
         mm(R("p1", 0, L), R("NI"), R("FY"), False, True)
-        mm(R("p5", 0, L), R("BO"), R("AE"))
-        lists2("p4", 0, "SQ", 24)
-        lists2("p3", 40, "SR", 24)
-        ts(R("F2"), R("E2"), 0.5, Op.mult, -0.25, Op.add)
-        ts(R("BR"), R("p5", 0, L), col("T2", 1), Op.is_le)
-        lists(R("p7", 0), "SU", "BR", 12)
+        act_lin(R("QR", 12, 24), R("p4", 12, 24), -1.0, 0.5)
         tt(R("p2", 0, L), R("F2"), R("BR"), Op.mult)
-        cp(R("QR", 24, 48), R("p3", 40, 64))
+        cp(R("QR", 36, 48), R("p3", 52, 64))
         tt(R("HS%d" % t), R("p2", 0, L), R("Q1"), Op.add)
+        cp(R("BRL"), R("p7", 0, 12))
         if not last:
             deps("G", [R("HS%d" % t)], [])
             g.remote_dma(ap(R("H%d" % (t + 1))), ap(R("HS%d" % t)), T.sem["ha%d" % (t + 1)], T.sem["loc"], pid, rid, mask)
         else:
             dma("S", T["yh"][:, :], ap(R("HS%d" % t)), [R("HS%d" % t)], [])
         if t == 0:
-            lists(R("p6", 0), "SY", "BMR", 12)
-        act_lin(R("QR", 0, 24), R("p4", 0, 24), -1.0, 0.5)
-        for j in range(24):
-            if j == 10:
-                cp(R("BRL"), R("p7", 0, 12))
-            if j >= NQ:
-                act_bias(R("OQ", QW * j, QW * j + 129), R("IQ"), Act.Sign, col("QR", j))
-            else:
-                ts(R("OQ", QW * j, QW * j + 129), R("IQ"), col("QR", j), Op.add, 0.0, Op.is_gt)
-            if j < 12:
-                ts(R("OR", 128 * j, 128 * j + 128), R("BD"), col("QR", 24 + j), Op.is_equal)
-            else:
-                ts(R("OR", 128 * j, 128 * j + 128), R("BD"), col("QR", 24 + j), Op.is_equal, col("BRL", j - 12), Op.mult)
-        tt(R("GF"), R("p1", 0, L), R("BR"), Op.mult)
-        if t == 0:
             cp(R("BU"), R("p6", 0, 12))
+            agather(R("FB"), R("TF", 0, P), R("BU"))
+        for j in range(24 - NQ, 24):
+            steps(j)
+        for j in range(12, 24):
+            if j < 24 - NQ:
+                steps(j)
+            one_hot(j)
+        products(12, 24)
+        tt(R("GF"), R("p1", 0, L), R("BR"), Op.mult)
         if not last:
-            for r in range(16):
-                mm(R("p5", 256, 268), R("SY", 128 * r, 128 * r + 128), R("FY", r, L, 16), r == 0, False)
-        for j in range(24):
-            mm(R("p0", 0, 129), R("OR", 128 * j, 128 * j + 128), R("OQ", QW * j, QW * j + 129), j == 0, j == 23)
-        if not last:
-            for r in range(16):
-                mm(R("p5", 256, 268), R("SY", 128 * r, 128 * r + 128), R("GF", r, L, 16), False, r == 15)
-            lists(R("p4", 100), "SN", "GF", 12)
+            for k, src in enumerate(("FY", "GF")):
+                for r in range(16):
+                    mm(R("p5", 256, 268), R("SY", 128 * r, 128 * r + 128), R(src, r, L, 16), k == 0 and r == 0, k == 1 and r == 15)
             if t == 0:
-                bookmarks()
+                bookmark_fields()
                 bookmark_lists()
-        cp(R("CS"), R("p0", 0, 128))
-        tt(R("MK"), R("p0", 1, 129), R("CS"), Op.is_gt)
-        tt(R("p2", 0, 128), R("MK"), DJ, Op.mult)
-        tt(R("ZF"), R("p2", 0, 128), R("JL"), Op.add)
-        cp(R("ZU"), R("ZF"))
+            lists(R("p4", 100), "SN", "GF", 12)
+        hs = ((64, 128), (0, 64))
+        for a, b in hs:
+            cp(R("CS", a, b), R("p0", a, b))
+        for a, b in hs:
+            tt(R("MK", a, b), R("p0", a + 1, b + 1), R("CS", a, b), Op.is_gt)
+        for a, b in hs:
+            tt(R("p2", a, b), R("MK", a, b), R("p2", 384 + a, 384 + b), Op.mult)
+        for a, b in hs:
+            tt(R("ZF", a, b), R("p2", a, b), R("JL", a, b), Op.add)
+        for a, b in hs:
+            cp(R("ZU", a, b), R("ZF", a, b))
         s1, s2, s3 = SPLIT
         if last:
             s1 = LAST1
         agather(R("B1", 16 * s1, P), R("BB"), R("ZU", s1, 128))
         if not last:
             if t == 0:
+                vgather(R("B1", 0, 16 * s1), R("BB"), R("ZU", 0, s1))
                 missed()
             tt(R("YF"), R("p5", 256, 268), R("YM", 0, 12), Op.add)
             tt(R("BN"), R("p3", 16, 28), R("YM", 12, 24), Op.add)
@@ -525,7 +561,8 @@ def rank_program(g, core, T, topo):
             deps("G", [R("KS%d" % t)], [])
             g.remote_dma(ap(R("K%d" % (t + 1))), ap(R("KS%d" % t)), T.sem["ka%d" % (t + 1)], T.sem["loc"], pid, rid, mask)
             tt(R("BF"), R("p4", 100, 112), R("BN"), Op.add)
-        vgather(R("B1", 0, 16 * s1), R("BB"), R("ZU", 0, s1))
+        if t:
+            vgather(R("B1", 0, 16 * s1), R("BB"), R("ZU", 0, s1))
         if last:
             mm(R("p5", 0, L), R("WNR"), R("FY"), True, False)
             mm(R("p5", 0, L), R("WNR"), R("GF"), False, True)
@@ -555,16 +592,24 @@ def rank_program(g, core, T, topo):
                 mm(R(b), R("ID"), R("XV", 512 * j, 512 * j + 512), True, False)
             for r in range(16):
                 mm(R(b, r, 512, 16), R("MT", 128 * r, 128 * r + 128), R("MK", 32 * j, 32 * j + 32), j < 2, j < 2 or r == 15)
-        for b, q0, q1 in (("p7", s3, 128), ("p5", 0, s3)):
+        for b, q0, q1 in (("p5", 0, s3), ("p7", s3, 128)):
             for r in range(16):
                 mm(R(b, q0, q1), R("SY", 128 * r, 128 * r + 128), R("TF", 16 * q0 + r, 16 * q1, 16), r == 0, r == 15)
         for j in (2, 3):
             act(R("XV", 512 * j, 512 * j + 512), R("p%d" % (1 + j)))
         tt(R("XV", 0, 512), R("XV", 0, 512), R("p1"), Op.add)
         tt(R("XV", 512, 1024), R("XV", 512, 1024), R("p2"), Op.add)
-        cp(R("JU", s3, 128), R("p7", s3, 128))
+        h1 = "H%d" % (t + 1)
+        cnt = len(topo.engines(prv, core))
+        arrive(h1, "ha%d" % (t + 1), cnt)
+        arrive("K%d" % (t + 1), "ka%d" % (t + 1), cnt)
+        for k in range(GK):
+            asel(R("HX", k, NX * 16, 16), R(h1, 0, NX), [[0, NX]], Op.is_ge, 0.0, 1, 0)
+        for k in range(GK, 16):
+            cp(R("HX", k, NX * 16, 16), R(h1, 0, NX))
         cp(R("JU", 0, s3), R("p5", 0, s3))
         cp(R("BU"), R("BF"))
+        cp(R("JU", s3, 128), R("p7", s3, 128))
         vgather(R("TX", 0, 16 * s3), R("XV"), R("JU", 0, s3))
         agather(R("TX", 16 * s3, P), R("XV"), R("JU", s3, 128))
         for b in range(6):

from concourse.mybir import AluOpType as Op, ActivationFunctionType as Act

BIG = 1.0e9
VOID = 640.0
L, P, NV = 192, 2048, 5
HS = P
VO = P + L
TW = VO + 16
NX = 128
CB = L - NX
CHUNKS = (0, 64, 128)
QW = 130
PRE = 5
NQ = 5
LAST1 = 60
SPLIT = (50, 60, 60)
GK = 9

B16, F32, I32, U16 = "bfloat16", "float32", "int32", "uint16"
SCRATCH = {
    "TX": ("sbuf", [128, TW], B16), "XV": ("sbuf", [128, P], B16), "TF": ("sbuf", [128, TW], B16),
    "BB": ("sbuf", [128, P], B16), "B1": ("sbuf", [128, P], B16), "PL": ("sbuf", [128, P], I32),
    "HX": ("sbuf", [128, NX * 16], B16), "DX": ("sbuf", [128, NX * 16], B16), "AX": ("sbuf", [128, NX * 16], B16),
    "GB": ("sbuf", [128, CB * 16], B16), "AB": ("sbuf", [128, CB * 16], B16),
    "KI": ("sbuf", [128, L], I32), "KA": ("sbuf", [128, 2 * L], I32), "KAB": ("sbuf", [128, 2 * L], F32),
    "VT": ("sbuf", [128, 2 * L], F32), "MS": ("sbuf", [128, 2 * L], F32), "RST": ("sbuf", [128, 2 * L], F32), "RS0": ("sbuf", [128, 2 * L], F32),
    "MI": ("sbuf", [128, 24], I32), "ML": ("sbuf", [128, 24], I32), "LB": ("sbuf", [128, 24], B16), "MV": ("sbuf", [128, 12], B16),
    "L1": ("sbuf", [128, 12], U16), "MISS": ("sbuf", [128, 12], F32), "CV": ("sbuf", [128, 24], F32), "SEL": ("sbuf", [128, 24], F32),
    "IV": ("sbuf", [128, 12], I32), "IX": ("sbuf", [128, 24], I32),
    "SI": ("sbuf", [128, L], I32), "Q1": ("sbuf", [128, L], I32), "FF": ("sbuf", [128, 3 * L], B16),
    "M1": ("sbuf", [128, 12], U16), "E2": ("sbuf", [128, L], B16), "AE": ("sbuf", [128, L], B16), "F2": ("sbuf", [128, L], I32),
    "BR": ("sbuf", [128, L], B16), "QR": ("sbuf", [128, 48], F32), "BRL": ("sbuf", [128, 12], F32),
    "BN": ("sbuf", [128, 12], F32), "YM": ("sbuf", [128, 24], F32),
    "YF": ("sbuf", [128, 12], F32), "YU": ("sbuf", [128, 12], U16), "BF": ("sbuf", [128, 12], F32), "BU": ("sbuf", [128, 12], U16),
    "JB": ("sbuf", [128, 24], F32), "FB": ("sbuf", [128, L], B16),
    "OR": ("sbuf", [128, 24 * 128], B16), "OQ": ("sbuf", [128, 24 * QW], B16), "CS": ("sbuf", [128, 128], F32),
    "MK": ("sbuf", [128, 128], B16), "JL": ("sbuf", [128, 128], F32), "NL": ("sbuf", [128, 128], F32),
    "ZF": ("sbuf", [128, 128], F32), "ZU": ("sbuf", [128, 128], U16), "JU": ("sbuf", [128, 128], U16),
    "AI": ("sbuf", [128, 2], I32), "AJ": ("sbuf", [128, 2], I32), "AK": ("sbuf", [128, 2], F32), "THR": ("sbuf", [128, 2], F32),
    "T1K": ("sbuf", [128, 2], F32), "T2": ("sbuf", [128, 2], F32),
    "ROW": ("sbuf", [128, P], F32), "RB": ("sbuf", [128, 4 * L], F32),
    "BD": ("sbuf", [128, 128], B16), "ONE": ("sbuf", [128, 128], B16), "ZER": ("sbuf", [128, 128], B16), "ON2": ("sbuf", [128, L], B16),
    "ID": ("sbuf", [128, 128], B16), "NI": ("sbuf", [128, 128], B16), "SP": ("sbuf", [128, 128], B16), "SM": ("sbuf", [128, 128], B16),
    "N32": ("sbuf", [128, 128], B16), "KBM": ("sbuf", [128, 128], B16), "BO": ("sbuf", [128, 128], B16),
    "WYR": ("sbuf", [128, 128], B16), "WNR": ("sbuf", [128, 128], B16), "IQ": ("sbuf", [128, 129], B16),
    "SU": ("sbuf", [128, 2048], B16), "SY": ("sbuf", [128, 2048], B16), "SN": ("sbuf", [128, 2048], B16), "SQ": ("sbuf", [128, 2048], B16),
    "SR": ("sbuf", [128, 2048], B16), "MT": ("sbuf", [128, 2048], B16), "PP": ("sbuf", [128, 8 * 128], B16),
    "CO": ("sbuf", [128, 16], F32), "CT": ("sbuf", [128, 16], F32), "RC": ("sbuf", [128, 16], F32), "R16": ("sbuf", [128, 16], F32),
    "IP": ("sbuf", [128, 2], I32), "IW": ("sbuf", [128, 2], I32), "IL": ("sbuf", [128, 128], I32), "I12": ("sbuf", [128, 12], I32), "IC": ("sbuf", [128, 128], I32),
    "CF": ("sbuf", [128, 4 * 128], B16), "CW": ("sbuf", [128, 4 * 128], I32), "NXC": ("sbuf", [128, 128], I32), "ICm": ("sbuf", [128, 128], I32),
    "BMC": ("sbuf", [128, 12], I32), "BMw": ("sbuf", [128, 24], I32), "BMf": ("sbuf", [128, 24], B16), "BMR": ("sbuf", [128, L], B16),
    "TH": ("sbuf", [128, 2], I32), "THw": ("sbuf", [128, 4], I32), "THf": ("sbuf", [128, 4], B16),
    "TSR": ("sbuf", [128, 128], B16), "TSx": ("sbuf", [128, 128], B16), "TS0": ("sbuf", [128, 128], B16), "TS1": ("sbuf", [128, 128], B16),
    "TMP": ("sbuf", [128, 512], B16),
    "HH": ("sbuf", [128, 2 * NV * L], B16), "KK": ("sbuf", [128, 2 * NV * L], U16),
}
ALIAS = {}
for _t in range(NV):
    ALIAS["H%d" % _t] = ("HH", L * _t, L)
    ALIAS["HS%d" % _t] = ("HH", L * (NV + _t), L)
    ALIAS["K%d" % _t] = ("KK", L * _t, L)
    ALIAS["KS%d" % _t] = ("KK", L * (NV + _t), L)
for _k, _n in enumerate(("BD0", "BD1", "N3a", "N3b")):
    ALIAS[_n] = ("TMP", 128 * _k, 128)
for _k, _n in enumerate(("FY", "FN", "GF")):
    ALIAS[_n] = ("FF", L * _k, L)
for _t in range(8):
    SCRATCH["p%d" % _t] = ("psum", [128, 512], F32)
NDMA = 32
SEMAPHORES = ["sV", "sA", "sT", "sG", "loc"] + ["d%d" % k for k in range(NDMA)] + ["ha%d" % t for t in range(1, NV)] + ["ka%d" % t for t in range(1, NV)]


def make_emitter(g, T):
    queues = {"V": g.vector, "A": g.scalar, "T": g.tensor, "G": g, "S": g.sync, "C": g.scalar}
    hist, know, snap, count, nd = {}, {}, {}, {}, [0]

    def ap(r):
        name, c0, c1, st, p = r
        return T[name][p, c0:c1:st] if st != 1 else T[name][p, c0:c1]

    def clash(a, b):
        if a[1] >= b[2] or b[1] >= a[2]:
            return False
        if a[3] == b[3] and a[3] > 1 and (a[1] - b[1]) % a[3]:
            return False
        if a[4] != b[4] and a[4].step is not None and a[4].step == b[4].step and a[4].start != b[4].start:
            return False
        return True

    def await_(q, sem, val):
        k = know.setdefault(q, {})
        if k.get(sem, 0) >= val:
            return
        queues[q].wait_ge(T.sem[sem], val)
        for s, v in snap.get((sem, val), {}).items():
            if v > k.get(s, 0):
                k[s] = v
        k[sem] = val

    def deps(q, reads, writes):
        need = {}
        for w, rs in ((False, reads), (True, writes)):
            for r in rs:
                psum = SCRATCH.get(r[0], ("",))[0] == "psum"
                for (h, hw, hq, sem, val) in hist.get(r[0], []):
                    if psum and hq != q:
                        hit = True
                    else:
                        hit = (w or hw) and clash(r, h)
                        if hit and psum and q == "T":
                            hit = False
                    if hit and val > need.get(sem, 0):
                        need[sem] = val
        for sem in sorted(need):
            await_(q, sem, need[sem])

    def note(q, reads, writes, sem, val):
        for w, rs in ((False, reads), (True, writes)):
            for r in rs:
                h = hist.setdefault(r[0], [])
                if w and r[0][0] != "p":
                    h[:] = [e for e in h if not (r[1] <= e[0][1] and r[2] >= e[0][2] and r[3] == 1 and r[4] == slice(None) and (e[2] != q or e[1]))]
                h[:] = [e for e in h if not (e[2] == q and e[1] == w and e[0] == r)]
                h.append((r, w, q, sem, val))

    def op(q, fn, reads, writes):
        deps(q, reads, writes)
        sem = "s" + q
        count[q] = count.get(q, 0) + 1
        fn(queues[q]).then_inc(T.sem[sem], 1)
        k = dict(know.setdefault(q, {}))
        k[sem] = count[q]
        snap[(sem, count[q])] = k
        note(q, reads, writes, sem, count[q])

    def dma(q, out, in_, reads, writes):
        kq = "A" if q == "C" else q
        deps(kq, reads, writes)
        sem = "d%d" % nd[0]
        nd[0] += 1
        queues[q].dma_start(out, in_).then_inc(T.sem[sem], 16)
        snap[(sem, 16)] = dict(know.setdefault(kq, {}))
        note("D" + sem, reads, writes, sem, 16)

    def arrive(name, sem, val):
        note("R" + sem, [], [R(name)], sem, val)

    def finish():
        for q in ("V", "A", "T", "G"):
            if count.get(q):
                await_("G", "s" + q, count[q])
        for k in range(nd[0]):
            await_("G", "d%d" % k, 16)

    return ap, op, dma, arrive, deps, finish


def R(name, c0=0, c1=None, st=1, p=slice(None)):
    if name in ALIAS:
        base, off, w = ALIAS[name]
        return (base, off + c0, off + (w if c1 is None else c1), st, p)
    return (name, c0, SCRATCH[name][1][1] if c1 is None else c1, st, p)


def col(name, j):
    return R(name, j, j + 1)


def rank_program(g, core, T, topo):
    rank = T.rank_of(core)
    if rank is None:
        return
    n = len(T.cores)
    nxt, prv = T.cores[(rank + 1) % n], T.cores[(rank - 1) % n]
    rid, pid = topo.addr(nxt, core)
    mask = topo.mask(core, nxt)
    ap, op, dma, arrive, deps, finish = make_emitter(g, T)

    def tt(out, a, b, o):
        op("V", lambda e: e.tensor_tensor(ap(out), ap(a), ap(b), o), [a, b], [out])

    def ts(out, a, s1, o0, s2=None, o1=None):
        rd = [a] + [s for s in (s1, s2) if isinstance(s, tuple)]
        v1 = ap(s1) if isinstance(s1, tuple) else s1
        v2 = ap(s2) if isinstance(s2, tuple) else s2
        if o1 is None:
            op("V", lambda e: e.tensor_scalar(ap(out), ap(a), v1, None, o0), rd, [out])
        else:
            op("V", lambda e: e.tensor_scalar(ap(out), ap(a), v1, v2, o0, o1), rd, [out])

    def cp(out, a):
        op("V", lambda e: e.tensor_copy(ap(out), ap(a)), [a], [out])

    def fill(out, c):
        op("V", lambda e: e.memset(ap(out), c), [], [out])

    def act(out, a, f=Act.Copy):
        op("A", lambda e: e.activation(ap(out), ap(a), f), [a], [out])

    def act_bias(out, a, f, b):
        op("A", lambda e: e.activation(ap(out), ap(a), f, bias=ap(b)), [a, b], [out])

    def act_lin(out, a, sc, bs):
        op("A", lambda e: e.activation(ap(out), ap(a), Act.Copy, bias=bs, scale=sc), [a], [out])

    def act_scale(out, a, c):
        op("A", lambda e: e.activation(ap(out), ap(a), Act.Copy, scale=ap(c)), [a, c], [out])

    def vgather(out, win, off):
        op("V", lambda e: e.tensor_copy(ap(out), ap(win).indirect(ap(off))), [win, off], [out])

    def agather(out, win, off):
        op("A", lambda e: e.activation(ap(out), ap(win).indirect(ap(off)), Act.Copy), [win, off], [out])

    def ttgather(out, win, off, b, o):
        op("V", lambda e: e.tensor_tensor(ap(out), ap(win).indirect(ap(off)), ap(b), o), [win, off, b], [out])

    def mm(out, lhs, rhs, start=True, stop=True):
        op("T", lambda e: e.matmul(ap(out), ap(lhs), ap(rhs), start, stop), [lhs, rhs], [out])

    def iota(out, pat, base, cm):
        small = SCRATCH[out[0]][2] != I32
        op("G", lambda e: e.iota(ap(out), pat, base, cm, allow_small_or_imprecise_dtypes=True) if small else e.iota(ap(out), pat, base, cm), [], [out])

    def asel(out, a, pat, o, fv, base, cm):
        op("G", lambda e: e.affine_select(ap(out), ap(a), pat, o, fv, base, cm), [a], [out])

    def lists(out, S, src, width):
        for r in range(16):
            mm(R(out[0], out[1], out[1] + width), R(S, 128 * r, 128 * r + 128), R(src, r, 16 * width, 16), r == 0, r == 15)

    def lists2(bank, c, S, width):
        for r in range(16):
            mm(R(bank, c, c + width), R(S, 128 * r, 128 * r + 128), R("FF", r, 16 * width, 16), r == 0, r == 15)

    DJ = R("p2", 384, 512)

    dma("S", T["KI"][:, :], T["kt"][:, :], [], [R("KI")])
    dma("C", T["NXC"][:, :], T["nx"][:, :], [], [R("NXC")])
    dma("S", ap(R("H0")), T["hm"][:, :], [], [R("H0")])
    dma("S", T["TX"][:, 0:P], T["xp"][:, :], [], [R("TX", 0, P)])
    dma("C", T["TH"][0:8, :], T["th"][:, :], [], [R("TH")])
    dma("C", T["BMC"][:, :], T["bm"][:, :], [], [R("BMC")])
    dma("S", T["XV"][:, :], T["xp"][:, :], [], [R("XV")])
    dma("S", T["PL"][:, :], T["pl"][:, :], [], [R("PL")])

    fill(R("ONE"), 1.0)
    fill(R("ON2"), 1.0)
    fill(R("ZER"), 0.0)
    iota(R("IP"), [[0, 2]], 0, 1)
    iota(R("BD0"), [[0, 8], [1, 16]], 0, 0)
    asel(R("BD1"), R("BD0"), [[-16, 8], [0, 16]], Op.is_ge, -1.0, 0, 1)
    asel(R("BD"), R("BD1"), [[16, 8], [0, 16]], Op.is_ge, -1.0, 15, -1)
    asel(R("ID"), R("ONE"), [[-1, 128]], Op.is_equal, 0.0, 0, 1)
    iota(R("IC"), [[1, 128]], 0, 128)
    iota(R("I12"), [[32, 6], [0, 2]], 0, 0)
    asel(R("SP"), R("ONE"), [[-1, 128]], Op.is_equal, 0.0, 16, 1)
    asel(R("SM"), R("ONE"), [[-1, 128]], Op.is_equal, 0.0, -16, 1)
    e8 = slice(0, 8)
    asel(R("TSx", p=e8), R("ONE", p=e8), [[1, 128]], Op.is_ge, 0.0, 0, -16)
    asel(R("TSR", p=e8), R("TSx", p=e8), [[-1, 128]], Op.is_ge, 0.0, 15, 16)
    asel(R("TS0", p=e8), R("ONE", p=e8), [[-2, 4], [0, 32]], Op.is_equal, 0.0, 0, 1)
    asel(R("TS1", p=e8), R("ONE", p=e8), [[-2, 4], [0, 32]], Op.is_equal, 0.0, -1, 1)
    iota(R("IQ"), [[1, 129]], -129, 0)
    iota(R("R16"), [[1, 16]], 0, 0)
    iota(R("IL"), [[16, 128]], 0, 0)
    asel(R("N3a"), R("ONE"), [[-32, 4], [0, 32]], Op.is_ge, 0.0, 0, 1)
    asel(R("N3b"), R("N3a"), [[32, 4], [0, 32]], Op.is_ge, 0.0, 31, -1)

    PM, RM1, RM0 = col("CO", 0), col("CO", 1), col("CO", 2)
    WY, WN, WQ, K64, W140, P32 = (col("CO", j) for j in range(3, 9))
    ts(R("IW", 0, 1), R("IP", 0, 1), 15, Op.bitwise_and)
    ts(R("IW", 1, 2), R("IP", 1, 2), 31, Op.bitwise_and)
    cp(PM, R("IW", 0, 1))
    for j, (f, w) in enumerate(((0, 16.0), (1, 1.0), (2, 16.0), (3, 1.0), (0, 1.0), (4, -128.0), (1, 1.0))):
        ts(col("CT", j), PM, float(f), Op.is_equal, w, Op.mult)
    tt(WY, col("CT", 0), col("CT", 1), Op.add)
    tt(WN, col("CT", 2), col("CT", 3), Op.add)
    tt(WQ, col("CT", 4), col("CT", 5), Op.add)
    for j, w in enumerate((WN, col("CT", 6), WQ)):
        ts(col("CT", 8 + j), w, 1.0 / 1024, Op.mult)
    ts(K64, PM, 64.0, Op.mult)
    for r in range(16):
        ts(R("SU", 128 * r, 128 * r + 128), R("BD"), float(r), Op.is_equal, 1024.0, Op.mult)
    act_scale(R("SN"), R("SU"), col("CT", 8))
    act_scale(R("SR"), R("SU"), col("CT", 9))
    ts(R("CW", 256, 384), R("NXC"), 4, Op.logical_shift_right)
    ts(R("CW", 384, 512), R("NXC"), 15, Op.bitwise_and)
    ts(R("ICm"), R("IC"), P - 1, Op.bitwise_and)
    ts(R("CW", 0, 128), R("ICm"), 4, Op.logical_shift_right)
    ts(R("CW", 128, 256), R("ICm"), 15, Op.bitwise_and)
    cp(R("CF"), R("CW"))
    for f in range(16):
        src = R("CF", 128 * f, 128 * f + 128) if f < 4 else R("ONE" if f == 4 else "ZER")
        dst = R("TF", 0, P, 1, slice(f, 128, 16))
        dma("S", ap(dst), ap(src), [src], [dst])
    cp(R("K0"), R("KI"))
    for k in range(16):
        cp(R("HX", k, NX * 16, 16), R("H0", 0, NX))
    ts(R("THw", 0, 2, 1, e8), R("TH", 0, 2, 1, e8), 4032, Op.bitwise_and)
    ts(R("THw", 2, 4, 1, e8), R("TH", 0, 2, 1, e8), 63, Op.bitwise_and)
    cp(R("THf", 0, 4, 1, e8), R("THw", 0, 4, 1, e8))
    for j in range(2):
        mm(R("p7", 200, 202), R("TSR", p=e8), R("THf", 2 * j, 2 * j + 2, 1, e8), j == 0, j == 1)
    for s in range(2):
        for j in range(2):
            mm(R("p7", 202 + s, 203 + s), R("TS%d" % s, p=e8), R("THf", 2 * j, 2 * j + 1, 1, e8), j == 0, j == 1)
    ts(R("KBM"), R("ID"), K64, Op.mult)
    ts(R("NI"), R("ID"), -1.0, Op.mult)

    def more_constants():
        ts(R("BO"), R("BD"), 0.0, Op.is_ge)
        cp(P32, R("IW", 1, 2))
        ts(R("RC"), R("R16"), PM, Op.is_equal, VOID, Op.mult)
        ts(R("WYR"), R("BO"), WY, Op.mult)
        ts(R("IV"), R("I12"), P32, Op.add)
        act_scale(R("SQ"), R("SU"), col("CT", 10))
        for r in range(16):
            act_scale(R("MT", 128 * r, 128 * r + 128), R("BO"), col("RC", r))
        lists(R("p2", 0), "SN", "TF", 128)
        act(R("NL"), R("p2", 0, 128))
        fill(R("TF", VO, TW), 0.0)
        iota(R("RS0"), [[0, 2 * L]], 2 ** 24 - 1, 0)
        asel(R("RST"), R("RS0"), [[0, 24], [1, 16]], Op.is_equal, -BIG, 0, 0)
        fill(R("TX", VO, TW), 1024.0)
        fill(R("BMR"), 0.0)
        ts(R("BMw", 0, 12), R("BMC"), 4, Op.logical_shift_right)
        ts(R("BMw", 12, 24), R("BMC"), 15, Op.bitwise_and)
        ts(R("IX", 0, 12), R("IV"), 63, Op.bitwise_and)
        ts(R("IX", 12, 24), R("IV"), 6, Op.logical_shift_right)
        ts(W140, PM, 2.0, Op.is_equal, float(VO // 16), Op.mult)
        cp(R("BMf"), R("BMw"))
        for f in range(2):
            src, dst = R("BMf", 12 * f, 12 * f + 12), R("BMR", 0, L, 1, slice(f, 128, 16))
            dma("S", ap(dst), ap(src), [src], [dst])
        ts(RM1, R("IW", 1, 2), 16.0, Op.is_ge)
        ts(RM0, R("IW", 1, 2), 16.0, Op.is_lt)
        ts(R("TF", HS, VO), R("ON2"), W140, Op.mult)
        ts(R("CV", 0, 12), R("IX", 0, 12), 64.0, Op.add)
        ts(R("CV", 12, 24), R("IX", 12, 24), float(HS // 64 - 1), Op.add)
        for w, wt in enumerate((1.0, 64.0)):
            for u in range(2):
                for s in range(2):
                    m = "ID" if u == s else ("SP" if s else "SM")
                    j = 4 * w + 2 * u + s
                    ts(R("PP", 128 * j, 128 * j + 128), R(m), RM1 if u else RM0, Op.mult, wt, Op.mult)
        cp(R("T2"), R("p7", 200, 202))
        ts(R("T1K"), R("p7", 202, 204), 1024.0, Op.mult)
        ts(R("THR"), R("p7", 202, 204), 1024.0, Op.mult)
        for r in range(16):
            asel(R("SY", 128 * r, 128 * r + 128), R("WYR"), [[0, 8], [1, 16]], Op.is_equal, 0.0, -r, 0)
        dma("S", ap(R("BB")), ap(R("TF", 0, P)), [R("TF", 0, P)], [R("BB")])

    def late_constants():
        ts(R("JL", 0, 64), R("IL", 0, 64), PM, Op.add)
        ts(R("JL", 64, 128), R("IL", 64, 128), PM, Op.add)
        ts(R("N32"), R("N3b"), -1.0, Op.mult)
        ts(R("WNR"), R("BO"), WN, Op.mult)

    def bookmarks():
        agather(R("FB"), R("TF", 0, P), R("BU"))
        bookmark_fields()

    def bookmark_fields():
        lists(R("p6", 100), "SY", "FB", 12)
        lists(R("p6", 112), "SN", "FB", 12)

    def bookmark_lists():
        act(R("JB", 0, 12), R("p6", 100, 112))
        act_lin(R("JB", 12, 24), R("p6", 112, 124), 1.0, -float(VO))

    for t in range(NV):
        last = t == NV - 1
        H, K = "H%d" % t, "K%d" % t
        if t:
            cp(R("KI"), R(K))
        agather(R("GB"), R("TX", 0, P), R(K, NX, L))
        nc = len(CHUNKS) - 1
        for c in range(nc):
            a, b = CHUNKS[c], CHUNKS[c + 1]
            ttgather(R("DX", 16 * a, 16 * b), R("TX", 0, P), R(K, a, b), R("HX", 16 * a, 16 * b), Op.subtract)

        def sums(i0, i1, *srcs):
            o = R("p0", i0, i1)
            mm(o, R("KBM"), R("ON2", 0, i1 - i0), True, False)
            for src in srcs:
                for k in range(16):
                    mm(o, R("SU", 128 * k, 128 * k + 128), src(k), False, k == 15 and src is srcs[-1])

        def sums_c(c):
            a, b = CHUNKS[c], CHUNKS[c + 1]
            if c == nc - 1:
                if t:
                    cp(R("AI"), R("p6", 200, 202))
                ts(R("AX", 16 * a, 16 * b), R("DX", 16 * a, 16 * b), -2.0, Op.mult, 0.0, Op.max)
                sums(a, b, lambda k: R("DX", 16 * a + k, 16 * b, 16), lambda k: R("AX", 16 * a + k, 16 * b, 16))
            else:
                act(R("AX", 16 * a, 16 * b), R("DX", 16 * a, 16 * b), Act.Abs)
                sums(a, b, lambda k: R("AX", 16 * a + k, 16 * b, 16))

        for k in range(16):
            o = R("p%d" % (1 + k // 8), (k % 8) * CB, (k % 8) * CB + CB)
            mm(o, R("ID"), R("GB", k, 16 * CB, 16), True, False)
            mm(o, R("NI"), R(H, NX, L), False, True)
        sums_c(0)
        for j in range(2):
            act(R("AB", 8 * CB * j, 8 * CB * j + 8 * CB), R("p%d" % (1 + j), 0, 8 * CB), Act.Abs)
        for c in range(nc - 1, 0, -1):
            sums_c(c)
        sums(NX, L, lambda k: R("AB", CB * k, CB * k + CB))
        act(R("TX", HS, VO), R(H))
        ts(R("KA", 0, L), R("KI"), 63, Op.bitwise_and)
        if t:
            ts(R("AJ"), R("AI"), 31, Op.bitwise_and)
        ts(R("KA", L, 2 * L), R("KI"), 6, Op.logical_shift_right)
        if t:
            ts(R("AK"), R("AJ"), 1024.0, Op.mult)
            tt(R("THR"), R("AK"), R("T1K"), Op.add)
            bookmarks()
            act(R("JL", SPLIT[2], 128), R("p7", SPLIT[2], 128))
            act(R("JL", 0, SPLIT[2]), R("p5", 0, SPLIT[2]))
            bookmark_lists()
        else:
            more_constants()
        def half(name, w):
            return R(name, L * w, L * w + L)

        def twelve(name, w):
            return R(name, 12 * w, 12 * w + 12)

        for w in range(2):
            tt(half("KAB", w), R("p0", 0, L), half("KA", w), Op.add)
        for w in range(2):
            op("V", lambda e: e.transpose(ap(half("VT", w)), ap(half("KAB", w))), [half("KAB", w)], [half("VT", w)])
        for w in range(2):
            op("V", lambda e: e.tensor_tensor_scan(ap(half("MS", w)), ap(half("RST", w)), ap(half("VT", w)), BIG, Op.max, Op.min), [half("RST", w), half("VT", w)], [half("MS", w)])
        cp(twelve("MI", 0), R("MS", 15, L, 16))
        for s in range(2):
            ts(R("MV", s, 12, 2), R("MS", 15 + 16 * s, L, 32), col("THR", s), Op.is_ge)
        cp(twelve("MI", 1), R("MS", L + 15, 2 * L, 16))
        ts(twelve("ML", 0), twelve("MI", 0), 63, Op.bitwise_and)
        for w in range(2):
            tt(twelve("SEL", w), R("MV"), twelve("CV", w), Op.mult)
        ts(twelve("ML", 1), twelve("MI", 1), 63, Op.bitwise_and)
        for w in range(2):
            tt(twelve("LB", w), twelve("ML", w), twelve("SEL", w), Op.max)
        for u in range(2):
            for w in range(2):
                for s in range(2):
                    j = 4 * w + 2 * u + s
                    mm(R("p3", u, 12, 2), R("PP", 128 * j, 128 * j + 128), R("LB", 12 * w + s, 12 * w + 12, 2), w == 0 and s == 0, w == 1 and s == 1)
        cp(R("L1"), R("p3", 0, 12))

        def missed():
            tt(R("YM", 0, 12), R("JB", 0, 12), R("MISS"), Op.mult)
            tt(R("YM", 12, 24), R("JB", 12, 24), R("MISS"), Op.mult)

        ttgather(R("SI"), R("TX", 0, VO), R("L1"), R(H), Op.add)
        agather(R("FY"), R("TF", 0, VO), R("L1"))
        ts(R("MISS"), R("p3", 0, 12), float(HS), Op.is_ge)
        ts(R("Q1"), R("SI"), 1, Op.arith_shift_right)
        if t and not last:
            missed()
        lists(R("p3", 16), "SN", "FY", 12)
        if t == 0:
            late_constants()
        tt(DJ, R("NL"), R("JL"), Op.subtract)
        cp(R("M1"), R("p3", 16, 28))
        ttgather(R("E2"), R("TX"), R("M1"), R("Q1"), Op.subtract)
        agather(R("FN"), R("TF"), R("M1"))
        act(R("AE"), R("E2"), Act.Abs)
        def one_hot(j):
            if j < 12:
                ts(R("OR", 128 * j, 128 * j + 128), R("BD"), col("QR", 24 + j), Op.is_equal)
            else:
                ts(R("OR", 128 * j, 128 * j + 128), R("BD"), col("QR", 24 + j), Op.is_equal, col("BRL", j - 12), Op.mult)

        def steps(j):
            if j < 24 - NQ:
                act_bias(R("OQ", QW * j, QW * j + 129), R("IQ"), Act.Sign, col("QR", j))
            else:
                ts(R("OQ", QW * j, QW * j + 129), R("IQ"), col("QR", j), Op.add, 0.0, Op.is_gt)

        def products(j0, j1):
            for j in range(j0, j1):
                mm(R("p0", 0, 129), R("OR", 128 * j, 128 * j + 128), R("OQ", QW * j, QW * j + 129), j == 0, j == 23)

        lists(R("p6", 140), "SR", "FY", 12)
        lists(R("p4", 0), "SQ", "FY", 12)
        mm(R("p5", 0, L), R("BO"), R("AE"))
        cp(R("QR", 24, 36), R("p6", 140, 152))
        ts(R("F2"), R("E2"), 0.5, Op.mult, -0.25, Op.add)
        act_lin(R("QR", 0, 12), R("p4", 0, 12), -1.0, 0.5)
        for j in range(12):
            steps(j)
        for j in range(PRE):
            one_hot(j)
        ts(R("BR"), R("p5", 0, L), col("T2", 1), Op.is_le)
        for j in range(PRE, 12):
            one_hot(j)
        lists(R("p4", 12), "SQ", "FN", 12)
        lists(R("p3", 52), "SR", "FN", 12)
        lists(R("p7", 0), "SU", "BR", 12)
        if t == 0:
            lists(R("p6", 0), "SY", "BMR", 12)
        products(0, 12)
        mm(R("p1", 0, L), R("ID"), R("FN"), True, False)
        mm(R("p1", 0, L), R("NI"), R("FY"), False, True)
        act_lin(R("QR", 12, 24), R("p4", 12, 24), -1.0, 0.5)
        tt(R("p2", 0, L), R("F2"), R("BR"), Op.mult)
        cp(R("QR", 36, 48), R("p3", 52, 64))
        tt(R("HS%d" % t), R("p2", 0, L), R("Q1"), Op.add)
        cp(R("BRL"), R("p7", 0, 12))
        if not last:
            deps("G", [R("HS%d" % t)], [])
            g.remote_dma(ap(R("H%d" % (t + 1))), ap(R("HS%d" % t)), T.sem["ha%d" % (t + 1)], T.sem["loc"], pid, rid, mask)
        else:
            dma("S", T["yh"][:, :], ap(R("HS%d" % t)), [R("HS%d" % t)], [])
        if t == 0:
            cp(R("BU"), R("p6", 0, 12))
            agather(R("FB"), R("TF", 0, P), R("BU"))
        for j in range(24 - NQ, 24):
            steps(j)
        for j in range(12, 24):
            if j < 24 - NQ:
                steps(j)
            one_hot(j)
        products(12, 24)
        tt(R("GF"), R("p1", 0, L), R("BR"), Op.mult)
        if not last:
            for k, src in enumerate(("FY", "GF")):
                for r in range(16):
                    mm(R("p5", 256, 268), R("SY", 128 * r, 128 * r + 128), R(src, r, L, 16), k == 0 and r == 0, k == 1 and r == 15)
            if t == 0:
                bookmark_fields()
                bookmark_lists()
            lists(R("p4", 100), "SN", "GF", 12)
        hs = ((64, 128), (0, 64))
        for a, b in hs:
            cp(R("CS", a, b), R("p0", a, b))
        for a, b in hs:
            tt(R("MK", a, b), R("p0", a + 1, b + 1), R("CS", a, b), Op.is_gt)
        for a, b in hs:
            tt(R("p2", a, b), R("MK", a, b), R("p2", 384 + a, 384 + b), Op.mult)
        for a, b in hs:
            tt(R("ZF", a, b), R("p2", a, b), R("JL", a, b), Op.add)
        for a, b in hs:
            cp(R("ZU", a, b), R("ZF", a, b))
        s1, s2, s3 = SPLIT
        if last:
            s1 = LAST1
        agather(R("B1", 16 * s1, P), R("BB"), R("ZU", s1, 128))
        if not last:
            if t == 0:
                vgather(R("B1", 0, 16 * s1), R("BB"), R("ZU", 0, s1))
                missed()
            tt(R("YF"), R("p5", 256, 268), R("YM", 0, 12), Op.add)
            tt(R("BN"), R("p3", 16, 28), R("YM", 12, 24), Op.add)
            cp(R("YU"), R("YF"))
            vgather(R("KS%d" % t), R("PL"), R("YU"))
            deps("G", [R("KS%d" % t)], [])
            g.remote_dma(ap(R("K%d" % (t + 1))), ap(R("KS%d" % t)), T.sem["ka%d" % (t + 1)], T.sem["loc"], pid, rid, mask)
            tt(R("BF"), R("p4", 100, 112), R("BN"), Op.add)
        if t:
            vgather(R("B1", 0, 16 * s1), R("BB"), R("ZU", 0, s1))
        if last:
            mm(R("p5", 0, L), R("WNR"), R("FY"), True, False)
            mm(R("p5", 0, L), R("WNR"), R("GF"), False, True)
            mm(R("p6", 0, L), R("WNR"), R("FB"))
            cp(R("RB", 0, L), R("p5", 0, L))
            tt(R("RB", L, 2 * L), R("p6", 0, L), R("RB", 0, L), Op.subtract)
            ts(R("RB", 2 * L, 3 * L), R("RB", 0, L), float(P), Op.is_ge)
        vgather(R("TF", 0, 16 * s2), R("B1"), R("ZU", 0, s2))
        agather(R("TF", 16 * s2, P), R("B1"), R("ZU", s2, 128))
        if last:
            tt(R("RB", 3 * L, 4 * L), R("RB", L, 2 * L), R("RB", 2 * L, 3 * L), Op.mult)
            tt(R("RB", L, 2 * L), R("RB", 3 * L, 4 * L), R("RB", 0, L), Op.add)
            src = R("RB", L, 2 * L, 1, slice(0, 128, 16))
            dma("S", T["yb"][:, :], ap(src), [src], [])
            for j in range(4):
                mm(R("p%d" % (1 + j), 0, 512), R("WYR"), R("TF", 512 * j, 512 * j + 512))
                if j % 2:
                    act(R("ROW", 512 * j, 512 * j + 512), R("p%d" % (1 + j)))
                else:
                    cp(R("ROW", 512 * j, 512 * j + 512), R("p%d" % (1 + j)))
            src = R("ROW", 0, P, 1, slice(0, 128, 16))
            dma("S", T["yj"][:, :], ap(src), [src], [])
            break
        for j in range(4):
            b = "p%d" % (1 + j)
            if j >= 2:
                mm(R(b), R("ID"), R("XV", 512 * j, 512 * j + 512), True, False)
            for r in range(16):
                mm(R(b, r, 512, 16), R("MT", 128 * r, 128 * r + 128), R("MK", 32 * j, 32 * j + 32), j < 2, j < 2 or r == 15)
        for b, q0, q1 in (("p5", 0, s3), ("p7", s3, 128)):
            for r in range(16):
                mm(R(b, q0, q1), R("SY", 128 * r, 128 * r + 128), R("TF", 16 * q0 + r, 16 * q1, 16), r == 0, r == 15)
        for j in (2, 3):
            act(R("XV", 512 * j, 512 * j + 512), R("p%d" % (1 + j)))
        tt(R("XV", 0, 512), R("XV", 0, 512), R("p1"), Op.add)
        tt(R("XV", 512, 1024), R("XV", 512, 1024), R("p2"), Op.add)
        h1 = "H%d" % (t + 1)
        cnt = len(topo.engines(prv, core))
        arrive(h1, "ha%d" % (t + 1), cnt)
        arrive("K%d" % (t + 1), "ka%d" % (t + 1), cnt)
        for k in range(GK):
            asel(R("HX", k, NX * 16, 16), R(h1, 0, NX), [[0, NX]], Op.is_ge, 0.0, 1, 0)
        for k in range(GK, 16):
            cp(R("HX", k, NX * 16, 16), R(h1, 0, NX))
        cp(R("JU", 0, s3), R("p5", 0, s3))
        cp(R("BU"), R("BF"))
        cp(R("JU", s3, 128), R("p7", s3, 128))
        vgather(R("TX", 0, 16 * s3), R("XV"), R("JU", 0, s3))
        agather(R("TX", 16 * s3, P), R("XV"), R("JU", s3, 128))
        for b in range(6):
            mm(R("p6", 200, 202), R("N32"), R("MV", 2 * b, 2 * b + 2), b == 0, b == 5)
    finish()
    g.wait_ge(T.sem["loc"], 2 * (NV - 1) * len(topo.engines(core, nxt)))
